import numpy as np
import ml_dtypes


def mxq(x, axis, fmt="e4m3"):
    dtype, down = {"e4m3": (ml_dtypes.float8_e4m3fn, 7), "e5m2": (ml_dtypes.float8_e5m2, 14)}[fmt]
    v = np.moveaxis(np.asarray(x, np.float32).astype(ml_dtypes.bfloat16).astype(np.float64), axis, -1)
    blocks = v.reshape(v.shape[:-1] + (-1, 32))
    amax = np.abs(blocks).max(-1, keepdims=True)
    byte = np.maximum(np.where(amax > 0, np.frexp(amax)[1] - 1 + 127, 0) - down, 1)
    scale = np.exp2(byte - 127.0)
    codes = (blocks / scale).astype(np.float32).astype(dtype).astype(np.float64)
    return np.moveaxis((codes * scale).reshape(v.shape), -1, axis)


WIDE = False


def mx_kscale(k):
    if not WIDE:
        return np.ones(k)
    levels = np.array([10, -10, 5, -5, 0])
    if k % 512:
        return np.exp2(np.random.permutation(np.resize(levels, k // 32))).repeat(32)
    a = np.empty((k // 512, 16))
    for p in range(k // 512):
        a[p, :8] = np.random.permutation(np.resize(levels, 8))
        for g in range(8):
            far = levels[np.abs(levels - a[p, g]) >= 10]
            a[p, g + 8] = far[np.random.randint(len(far))]
    return np.exp2(a.ravel()).repeat(32)


def f64(x):
    return np.asarray(x).astype(np.float64)


def striped(idx):
    return np.tile(idx.reshape(-1, 16).T, (8, 1)).astype(np.uint16)


def unstriped(offs):
    return offs[:16].T.reshape(-1).astype(np.int64)


E2M1 = np.array([0.0, 0.5, 1.0, 1.5, 2.0, 3.0, 4.0, 6.0, -0.0, -0.5, -1.0, -1.5, -2.0, -3.0, -4.0, -6.0])


def pack_weight(w, fmt):
    k, n = w.shape
    w = f64(np.asarray(w, np.float32).astype(ml_dtypes.bfloat16)).reshape(k // 32, 32, n)
    amax = np.abs(w).max(1)
    if fmt == "e4m3":
        byte = np.frexp(amax)[1] - 1 + 127 - 7
    else:
        mant, ex = np.frexp(amax / 6.0)
        byte = np.where(mant > 0.5, ex, ex - 1) + 127
    byte = np.clip(np.where(amax > 0, byte, 1), 1, 254)
    scaled = (w * np.exp2(127.0 - byte)[:, None, :]).reshape(k, n).astype(np.float32)
    by_word = np.ascontiguousarray(scaled.reshape(k // 512, 128, 4, n).transpose(0, 1, 3, 2))
    if fmt == "e4m3":
        words = by_word.astype(ml_dtypes.float8_e4m3fn).view(np.uint8)
    else:
        c = by_word.astype(ml_dtypes.float4_e2m1fn).view(np.uint8) & 0xF
        words = (c[..., 0::2] | (c[..., 1::2] << 4)).reshape(k // 512, 128, 2 * n)
    return np.ascontiguousarray(words), np.ascontiguousarray(byte.astype(np.uint8).reshape(k // 512, 16, n))


def unpack_weight(words, scales, fmt):
    g, _, n = scales.shape
    words = np.ascontiguousarray(words).reshape(g, 128, n, -1)
    if fmt == "e4m3":
        vals = words.view(ml_dtypes.float8_e4m3fn).astype(np.float64)
    else:
        nib = np.empty((g, 128, n, 4), np.uint8)
        nib[..., 0::2] = words & 0xF
        nib[..., 1::2] = words >> 4
        vals = E2M1[nib]
    vals = vals * np.repeat(np.exp2(scales.astype(np.float64) - 127.0), 8, axis=1)[..., None]
    return vals.transpose(0, 1, 3, 2).reshape(g * 512, n)


def relu2(v):
    return np.maximum(v, 0.0) ** 2


K, T, E, C, N = 2048, 768, 9, 256, 128
TOP = 3
K8 = 1024


def by_expert(wq, xq):
    return np.concatenate([wq[e].T @ xq[:, e * C:(e + 1) * C] for e in range(E)], axis=1)


def setup_inputs():
    n = np.random.standard_normal
    s = mx_kscale(K)[:, None]
    deal = np.repeat(np.arange(E), C).reshape(TOP, T)[:, np.random.permutation(T)]
    deal = np.take_along_axis(deal, np.argsort(np.random.rand(TOP, T), axis=0), axis=0)
    for _ in range(8):
        s_, t_ = np.random.permutation(T).reshape(2, -1); r = np.random.randint(TOP, size=T // 2); x, y = deal[r, s_].copy(), deal[r, t_].copy()
        ok = ~((deal[:, s_] == y).any(0) | (deal[:, t_] == x).any(0)); deal[r[ok], s_[ok]] = y[ok]; deal[r[ok], t_[ok]] = x[ok]
    order = np.lexsort((np.random.rand(TOP * T), deal.reshape(-1)))
    slot_token = order % T; pos = np.empty(TOP * T, np.int64); pos[order] = np.arange(TOP * T); pos = pos.reshape(TOP, T)
    g = np.random.uniform(0.5, 1.5, (TOP, T)); g = g / g.sum(0)
    w = n((E, K, N)) / np.sqrt(K) / s[None]
    w8 = [pack_weight(m[:K8], "e4m3") for m in w]
    w4 = [pack_weight(m[K8:], "e2m1") for m in w]
    return {
        "xT": (n((K, T)) * s).astype(np.float32),
        "w8_words": np.stack([m[0] for m in w8]),
        "w8_scales": np.stack([m[1] for m in w8]),
        "w4_words": np.stack([m[0] for m in w4]),
        "w4_scales": np.stack([m[1] for m in w4]),
        "b": (0.3 * n((N, E))).astype(np.float32),
        "gate": np.stack([np.tile(r, (N, 1)) for r in g]).astype(np.float32),
        "offs": striped(slot_token),
        "pos1": striped(pos[0]),
        "pos2": striped(pos[1]),
        "pos3": striped(pos[2]),
    }


def reference(xT, w8_words, w8_scales, w4_words, w4_scales, b, gate, offs, pos1, pos2, pos3):
    idx = unstriped(offs)
    w = np.stack([np.concatenate([unpack_weight(w8_words[e], w8_scales[e], "e4m3"), unpack_weight(w4_words[e], w4_scales[e], "e2m1")]) for e in range(E)])
    xq = mxq(f64(xT)[:, idx], 0, "e4m3")
    y = by_expert(w, xq)
    y = relu2(y + np.repeat(f64(b), C, axis=1))
    return sum(f64(gate[r]) * y[:, unstriped(p)] for r, p in enumerate((pos1, pos2, pos3)))

@@ -1,0 +1,217 @@
+from contextlib import ExitStack
+
+import concourse.mybir as mybir
+
+K, T, E, C, N = 2048, 768, 9, 256, 128
+SLOTS = E * C
+FLOPS = 2 * K * N * SLOTS
+
+F32 = mybir.dt.float32
+BF16 = mybir.dt.bfloat16
+I32 = mybir.dt.int32
+U32 = mybir.dt.uint32
+U16 = mybir.dt.uint16
+U8 = mybir.dt.uint8
+FP8X4 = mybir.dt.float8_e4m3fn_x4
+FP4X4 = mybir.dt.float4_e2m1fn_x4
+ACT = mybir.ActivationFunctionType
+ALU = mybir.AluOpType
+
+P = 128
+PASSES = 4
+PLANE = (4, 8, 0, 12)
+
+
+def tile_moe_tk_lin_relu2_kernel(
+    tc, xT, w8_words, w8_scales, w4_words, w4_scales, b, gate, offs, pos1, pos2, pos3, out
+):
+    nc = tc.nc
+    with ExitStack() as ctx:
+        held = ctx.enter_context(tc.tile_pool(name="held", bufs=1))
+        psum = ctx.enter_context(tc.psum_pool(name="psum", bufs=1))
+
+        offs_t = held.tile([P, SLOTS // 16], U16, name="offs_t")
+        pos_t = [held.tile([P, T // 16], U16, name=f"pos_t{r}") for r in range(3)]
+        x_f = [held.tile([P, 4, T], F32, name=f"x_f{a}") for a in range(PASSES)]
+        x_b = [
+            held.tile([P, T, 4], BF16, name=f"x_b{a}", tag="late" if a == 3 else f"x_b{a}", align_bytes=64)
+            for a in range(PASSES)
+        ]
+        x_w = {}
+        x_s = held.tile([P, T], U8, name="x_s", align_bytes=64)
+        g_w = {a: held.tile([P, SLOTS], U32, name=f"g_w{a}", align_bytes=64) for a in (0, 1, 3)}
+        g_w2 = [held.tile([P, 1024], U32, name="g_w2a", align_bytes=64)]
+        g_s = held.tile([P, SLOTS], U8, name="g_s", align_bytes=64)
+        m_s = held.tile([P, SLOTS], U8, name="m_s", align_bytes=64)
+        w8_t = held.tile([P, 2 * E, 4 * N], U8, name="w8_t", align_bytes=64)
+        w4_t = held.tile([P, 2 * E, 2 * N], U8, name="w4_t", align_bytes=64)
+        ws_t = held.tile([P, 2, 2 * E, N], U8, name="ws_t", align_bytes=64)
+        b_t = held.tile([P, E], F32, name="b_t")
+        gate_t = held.tile([P, 3, T], F32, name="gate_t")
+        relu_t = held.tile([P, SLOTS], F32, name="relu_t")
+        y_t = held.tile([P, SLOTS], F32, name="y_t")
+        pick = [held.tile([P, T], F32, name=f"pick{r}") for r in range(3)]
+        sum_t = held.tile([P, T], F32, name="sum_t")
+        out_t = held.tile([P, T], F32, name="out_t")
+        warm = held.tile([P, 1], F32, name="warm")
+        bank = [psum.tile([P, 512], F32, name=f"bank{i}") for i in range(8)]
+
+        nc.gpsimd.memset(x_s[:], 0)
+        nc.gpsimd.memset(m_s[:].bitcast(I32), 0)
+        nc.vector.memset(ws_t[:].rearrange("p s g n -> p (s g n)").bitcast(I32), 0)
+        nc.vector.memset(warm[:], 0.0)
+        nc.scalar.activation(warm[:], warm[:], ACT.Square)
+
+        xv = xT.rearrange("(a p j) t -> a p j t", a=PASSES, j=4)
+
+        def load_x(a, c0, c1):
+            nc.sync.dma_start(out=x_f[a][:, :, c0:c1], in_=xv[a, :, :, c0:c1])
+
+        def cast(engine, a, c0, c1):
+            src = x_f[a][:, :, c0:c1].rearrange("p j (c i) -> p c j i", i=4)
+            dst = x_b[a][:, c0:c1, :].rearrange("p (c i) j -> p c j i", i=4)
+            if engine == "v":
+                nc.vector.tensor_copy(dst, src)
+            else:
+                nc.scalar.activation(dst, src, ACT.Copy)
+
+        def quantise(a, c0, c1):
+            nc.vector.quantize_mx(
+                out=x_w[a][:, c0:c1].bitcast(FP8X4),
+                scales=x_s[PLANE[a] : P, c0:c1],
+                in_=x_b[a][:, c0:c1, :].rearrange("p t j -> p (t j)"),
+            )
+
+        def new_words(a):
+            x_w[a] = held.tile([P, T], U32, name=f"x_w{a}", align_bytes=64)
+
+        def words(a, s0, s1):
+            if a != 2:
+                return g_w[a][:, s0:s1]
+            return g_w2[0][:, s0:s1] if s1 <= 1024 else g_w2[1][:, s0 - 1024 : s1 - 1024]
+
+        def gather_words(a, s0, s1):
+            nc.vector.tensor_copy(words(a, s0, s1), x_w[a][:].indirect(offs_t[:, s0 // 16 : s1 // 16]))
+
+        def gather_scales(s0, s1):
+            nc.vector.tensor_copy(g_s[:, s0:s1], x_s[:].indirect(offs_t[:, s0 // 16 : s1 // 16]))
+
+        head_chunks = ((0, 384, 512), (512, 704, 768))
+        for c0, cm, c1 in head_chunks:
+            load_x(0, c0, c1)
+        nc.sync.dma_start(offs_t[:], offs)
+        for c0 in (0, 384):
+            load_x(1, c0, c0 + 384)
+        load_x(2, 0, T)
+        load_x(3, 0, T)
+        for s, scales in enumerate((w8_scales, w4_scales)):
+            for q in range(4):
+                nc.sync.dma_start(
+                    out=ws_t[32 * q : 32 * q + 4, s].bitcast(I32),
+                    in_=scales[:, :, 4 * q : 4 * q + 4, :].rearrange("e a q n -> q (e a) n").bitcast(I32),
+                )
+        nc.sync.dma_start(out=w8_t[:].bitcast(I32), in_=w8_words.rearrange("e a p n r -> p (e a) (n r)").bitcast(I32))
+        nc.sync.dma_start(out=w4_t[:].bitcast(I32), in_=w4_words.rearrange("e a p n -> p (e a) n").bitcast(I32))
+        nc.sync.dma_start(out=b_t[:], in_=b)
+        for t, src in zip(pos_t, (pos1, pos2, pos3)):
+            nc.sync.dma_start(t[:], src)
+        nc.sync.dma_start(out=gate_t[:], in_=gate.rearrange("r p t -> p r t"))
+
+        new_words(0)
+        for c0, cm, c1 in head_chunks:
+            cast("s", 0, cm, c1)
+            cast("v", 0, c0, cm)
+            quantise(0, c0, c1)
+        for a in (1, 2, 3):
+            cast("s", a, 0, 384)
+            cast("s", a, 384, 768)
+
+        def quantise_all(a):
+            new_words(a)
+            quantise(a, 0, 512)
+            quantise(a, 512, 768)
+
+        quarter = [(i * 576, (i + 1) * 576) for i in range(4)]
+        for a in (0, 1):
+            for s0, s1 in quarter[:3]:
+                gather_words(a, s0, s1)
+            new_words(a + 1)
+            quantise(a + 1, 0, 512)
+            gather_words(a, 1728, 2016)
+            quantise(a + 1, 512, 768)
+            gather_words(a, 2016, 2304)
+        gather_words(2, 0, 512)
+        quantise_all(3)
+        gather_words(2, 512, 1024)
+        for h0, h1 in ((0, 1152), (1152, 2304)):
+            for s0 in (h0, h0 + 576):
+                gather_scales(s0, s0 + 576)
+            for q in range(4):
+                nc.sync.dma_start(
+                    out=m_s[32 * q : 32 * q + 4, h0:h1].bitcast(I32),
+                    in_=g_s[32 * q + 12 : 32 * q + 16, h0:h1].bitcast(I32),
+                )
+        g_w2.append(held.tile([P, SLOTS - 1024], U32, name="g_w2b", tag="late", align_bytes=64))
+        def acc(g):
+            return bank[g % 8][:, (g // 8) * 128 : (g // 8 + 1) * 128]
+
+        def multiply(g, a):
+            e = g // 2
+            cols = slice(g * 128, (g + 1) * 128)
+            if a < 2:
+                lhsT = w8_t[:, 2 * e + a, :].bitcast(FP8X4)
+            else:
+                lhsT = w4_t[:, 2 * e + a - 2, :].bitcast(FP4X4)
+            nc.tensor.matmul_mx(
+                out=acc(g),
+                lhsT=lhsT,
+                lhsT_scale=ws_t[:, a // 2, 2 * e + a % 2, :],
+                rhs=words(a, cols.start, cols.stop).bitcast(FP8X4),
+                rhs_scale=m_s[:, cols] if a == 3 else g_s[PLANE[a] : P, cols],
+                start=(a == 0),
+                stop=(a == PASSES - 1),
+            )
+
+        def activate(g):
+            e = g // 2
+            if g == SLOTS // 128 - 1:
+                nc.vector.tensor_scalar(
+                    relu_t[:, g * 128 : (g + 1) * 128], acc(g), b_t[:, e : e + 1], 0.0, ALU.add, ALU.max
+                )
+                return
+            nc.scalar.activation(relu_t[:, g * 128 : (g + 1) * 128], acc(g), ACT.Relu, bias=b_t[:, e : e + 1])
+
+        def square(s0, s1):
+            nc.scalar.activation(y_t[:, s0:s1], relu_t[:, s0:s1], ACT.Square)
+
+        def open_groups(g0, g1):
+            for g in range(g0, min(g1, SLOTS // 128)):
+                multiply(g, 0)
+                multiply(g, 1)
+
+        open_groups(0, 8)
+        for s0, s1 in ((0, 512), (512, 1024), (1024, 1536), (1536, 2048), (2048, 2304)):
+            if s0 >= 1024:
+                gather_words(2, s0, s1)
+            for g in range(s0 // 128, s1 // 128):
+                multiply(g, 2)
+            pieces = ((s0, s1),) if s1 < SLOTS else ((s0, s0 + 128), (s0 + 128, s1))
+            for p0, p1 in pieces:
+                gather_words(3, p0, p1)
+                for g in range(p0 // 128, p1 // 128):
+                    multiply(g, 3)
+                    activate(g)
+            if s1 < SLOTS:
+                square(s0, s1)
+            else:
+                nc.vector.tensor_tensor(y_t[:, s0:s1], relu_t[:, s0:s1], relu_t[:, s0:s1], ALU.mult)
+            open_groups(s0 // 128 + 8, s1 // 128 + 8)
+
+        for r in range(3):
+            nc.vector.tensor_tensor(pick[r][:], y_t[:].indirect(pos_t[r][:]), gate_t[:, r, :], ALU.mult)
+        halves = ((0, 512), (512, 768))
+        for c0, c1 in halves:
+            nc.vector.tensor_tensor(sum_t[:, c0:c1], pick[0][:, c0:c1], pick[1][:, c0:c1], ALU.add)
+        for c0, c1 in halves:
+            nc.vector.tensor_tensor(out_t[:, c0:c1], sum_t[:, c0:c1], pick[2][:, c0:c1], ALU.add)
+            nc.sync.dma_start(out=out[:, c0:c1], in_=out_t[:, c0:c1])

@@ -1,6 +1,7 @@
 from contextlib import ExitStack
 
 import concourse.mybir as mybir
+from concourse.masks import make_identity
 
 K, T, E, C, N = 2048, 768, 9, 256, 128
 SLOTS = E * C
@@ -19,7 +20,16 @@ ALU = mybir.AluOpType
 
 P = 128
 PASSES = 4
+GROUPS = SLOTS // P
 PLANE = (4, 8, 0, 12)
+TURNED = 4
+TV = TURNED * P
+THIRDS = ((0, 256), (256, 512), (512, 768))
+WIDE = ((0, 512), (512, 768))
+LOADS = (THIRDS, THIRDS, WIDE, ((0, 768),))
+QUANT = (THIRDS, WIDE, WIDE, WIDE)
+HEAD_V = 160
+EARLY = 1024
 
 
 def tile_moe_tk_lin_relu2_kernel(
@@ -32,78 +42,97 @@ def tile_moe_tk_lin_relu2_kernel(
 
         offs_t = held.tile([P, SLOTS // 16], U16, name="offs_t")
         pos_t = [held.tile([P, T // 16], U16, name=f"pos_t{r}") for r in range(3)]
-        x_f = [held.tile([P, 4, T], F32, name=f"x_f{a}") for a in range(PASSES)]
-        x_b = [
-            held.tile([P, T, 4], BF16, name=f"x_b{a}", tag="late" if a == 3 else f"x_b{a}", align_bytes=64)
+        x_f = {
+            (a, c0): held.tile([P, 4, c1 - c0], F32, name=f"x_f{a}_{c0}", align_bytes=64)
             for a in range(PASSES)
-        ]
-        x_w = {}
-        x_s = held.tile([P, T], U8, name="x_s", align_bytes=64)
-        g_w = {a: held.tile([P, SLOTS], U32, name=f"g_w{a}", align_bytes=64) for a in (0, 1, 3)}
-        g_w2 = [held.tile([P, 1024], U32, name="g_w2a", align_bytes=64)]
+            for c0, c1 in LOADS[a]
+        }
+        x_b = {
+            (a, c0): held.tile([P, c1 - c0, 4], BF16, name=f"x_b{a}_{c0}", align_bytes=64)
+            for a in range(PASSES)
+            for c0, c1 in QUANT[a]
+        }
+        x_w = held.tile([P, (PASSES + 1) * T], I32, name="x_w", align_bytes=64)
+        x_s = held.tile([P, 2 * T], U8, name="x_s", align_bytes=64)
         g_s = held.tile([P, SLOTS], U8, name="g_s", align_bytes=64)
         m_s = held.tile([P, SLOTS], U8, name="m_s", align_bytes=64)
         w8_t = held.tile([P, 2 * E, 4 * N], U8, name="w8_t", align_bytes=64)
         w4_t = held.tile([P, 2 * E, 2 * N], U8, name="w4_t", align_bytes=64)
         ws_t = held.tile([P, 2, 2 * E, N], U8, name="ws_t", align_bytes=64)
         b_t = held.tile([P, E], F32, name="b_t")
-        gate_t = held.tile([P, 3, T], F32, name="gate_t")
+        gate_t = held.tile([P, 3, T - TV], F32, name="gate_t")
+        gate_rows = held.tile([P, P], F32, name="gate_rows")
+        gate_cols = held.tile([P, 3 * TURNED], F32, name="gate_cols")
+        ident = held.tile([P, P], F32, name="ident")
         relu_t = held.tile([P, SLOTS], F32, name="relu_t")
         y_t = held.tile([P, SLOTS], F32, name="y_t")
-        pick = [held.tile([P, T], F32, name=f"pick{r}") for r in range(3)]
-        sum_t = held.tile([P, T], F32, name="sum_t")
-        out_t = held.tile([P, T], F32, name="out_t")
+        pick = [held.tile([P, TV], F32, name=f"pick{r}") for r in range(3)]
+        scaled = [held.tile([P, TURNED, P], F32, name=f"scaled{r}") for r in range(3)]
+        prod = [held.tile([P, T - TV], F32, name=f"prod{r}") for r in range(3)]
+        sum_t = held.tile([P, T - TV], F32, name="sum_t")
+        out_a = held.tile([P, TV], F32, name="out_a")
+        out_b = held.tile([P, T - TV], F32, name="out_b")
         warm = held.tile([P, 1], F32, name="warm")
         bank = [psum.tile([P, 512], F32, name=f"bank{i}") for i in range(8)]
 
-        nc.gpsimd.memset(x_s[:], 0)
+        nc.gpsimd.memset(x_s[:].bitcast(I32), 0)
+        nc.gpsimd.memset(x_w[:, PASSES * T :], 0)
+        nc.gpsimd.memset(gate_rows[:], 0.0)
+        make_identity(nc, ident[:])
         nc.gpsimd.memset(m_s[:].bitcast(I32), 0)
-        nc.vector.memset(ws_t[:].rearrange("p s g n -> p (s g n)").bitcast(I32), 0)
         nc.vector.memset(warm[:], 0.0)
+        nc.vector.memset(ws_t[:].rearrange("p s g n -> p (s g n)").bitcast(I32), 0)
         nc.scalar.activation(warm[:], warm[:], ACT.Square)
 
         xv = xT.rearrange("(a p j) t -> a p j t", a=PASSES, j=4)
 
-        def load_x(a, c0, c1):
-            nc.sync.dma_start(out=x_f[a][:, :, c0:c1], in_=xv[a, :, :, c0:c1])
+        def load_x(a):
+            for c0, c1 in LOADS[a]:
+                nc.sync.dma_start(out=x_f[a, c0][:], in_=xv[a, :, :, c0:c1])
 
         def cast(engine, a, c0, c1):
-            src = x_f[a][:, :, c0:c1].rearrange("p j (c i) -> p c j i", i=4)
-            dst = x_b[a][:, c0:c1, :].rearrange("p (c i) j -> p c j i", i=4)
+            f0 = max(lo for lo, hi in LOADS[a] if lo <= c0)
+            b0 = max(lo for lo, hi in QUANT[a] if lo <= c0)
+            src = x_f[a, f0][:, :, c0 - f0 : c1 - f0].rearrange("p j (c i) -> p c j i", i=4)
+            dst = x_b[a, b0][:, c0 - b0 : c1 - b0, :].rearrange("p (c i) j -> p c j i", i=4)
             if engine == "v":
                 nc.vector.tensor_copy(dst, src)
             else:
                 nc.scalar.activation(dst, src, ACT.Copy)
 
+        def first_word(a):
+            return (PASSES - 1 - a) * T
+
         def quantise(a, c0, c1):
             nc.vector.quantize_mx(
-                out=x_w[a][:, c0:c1].bitcast(FP8X4),
+                out=x_w[:, first_word(a) + c0 : first_word(a) + c1].bitcast(FP8X4),
                 scales=x_s[PLANE[a] : P, c0:c1],
-                in_=x_b[a][:, c0:c1, :].rearrange("p t j -> p (t j)"),
+                in_=x_b[a, c0][:].rearrange("p t j -> p (t j)"),
             )
 
-        def new_words(a):
-            x_w[a] = held.tile([P, T], U32, name=f"x_w{a}", align_bytes=64)
+        g_w = {}
+
+        def new_words(a, s0, s1, tag=None):
+            name = f"g_w{a}_{s0}"
+            g_w[a, s0] = held.tile([P, s1 - s0], U32, name=name, tag=tag or name, align_bytes=64)
 
         def words(a, s0, s1):
-            if a != 2:
-                return g_w[a][:, s0:s1]
-            return g_w2[0][:, s0:s1] if s1 <= 1024 else g_w2[1][:, s0 - 1024 : s1 - 1024]
+            lo = max(first for pas, first in g_w if pas == a and first <= s0)
+            return g_w[a, lo][:, s0 - lo : s1 - lo]
 
         def gather_words(a, s0, s1):
-            nc.vector.tensor_copy(words(a, s0, s1), x_w[a][:].indirect(offs_t[:, s0 // 16 : s1 // 16]))
+            width = T if s1 - s0 <= 576 else 2 * T
+            window = x_w[:, first_word(a) : first_word(a) + width].bitcast(U32)
+            nc.vector.tensor_copy(words(a, s0, s1), window.indirect(offs_t[:, s0 // 16 : s1 // 16]))
 
-        def gather_scales(s0, s1):
-            nc.vector.tensor_copy(g_s[:, s0:s1], x_s[:].indirect(offs_t[:, s0 // 16 : s1 // 16]))
-
-        head_chunks = ((0, 384, 512), (512, 704, 768))
-        for c0, cm, c1 in head_chunks:
-            load_x(0, c0, c1)
+        load_x(0)
         nc.sync.dma_start(offs_t[:], offs)
-        for c0 in (0, 384):
-            load_x(1, c0, c0 + 384)
-        load_x(2, 0, T)
-        load_x(3, 0, T)
+        for a in (1, 2, 3):
+            load_x(a)
+        for r in range(3):
+            nc.sync.dma_start(
+                out=gate_rows[TURNED * r : TURNED * (r + 1), :], in_=gate[r, 0, 0:TV].rearrange("(c p) -> c p", p=P)
+            )
         for s, scales in enumerate((w8_scales, w4_scales)):
             for q in range(4):
                 nc.sync.dma_start(
@@ -115,49 +144,46 @@ def tile_moe_tk_lin_relu2_kernel(
         nc.sync.dma_start(out=b_t[:], in_=b)
         for t, src in zip(pos_t, (pos1, pos2, pos3)):
             nc.sync.dma_start(t[:], src)
-        nc.sync.dma_start(out=gate_t[:], in_=gate.rearrange("r p t -> p r t"))
+        nc.sync.dma_start(out=gate_t[:], in_=gate[:, :, TV:T].rearrange("r p t -> p r t"))
 
-        new_words(0)
-        for c0, cm, c1 in head_chunks:
-            cast("s", 0, cm, c1)
-            cast("v", 0, c0, cm)
+        for c0, c1 in THIRDS:
+            cast("s", 0, c0 + HEAD_V, c1)
+            cast("v", 0, c0, c0 + HEAD_V)
             quantise(0, c0, c1)
         for a in (1, 2, 3):
-            cast("s", a, 0, 384)
-            cast("s", a, 384, 768)
+            for c0, c1 in THIRDS if a == 1 else WIDE:
+                cast("s", a, c0, c1)
 
-        def quantise_all(a):
-            new_words(a)
-            quantise(a, 0, 512)
-            quantise(a, 512, 768)
+        nc.tensor.transpose(bank[7][:, 0:P], gate_rows[:], ident[:])
+        nc.scalar.copy(gate_cols[:], bank[7][:, 0 : 3 * TURNED])
 
-        quarter = [(i * 576, (i + 1) * 576) for i in range(4)]
-        for a in (0, 1):
-            for s0, s1 in quarter[:3]:
-                gather_words(a, s0, s1)
-            new_words(a + 1)
-            quantise(a + 1, 0, 512)
-            gather_words(a, 1728, 2016)
-            quantise(a + 1, 512, 768)
-            gather_words(a, 2016, 2304)
-        gather_words(2, 0, 512)
-        quantise_all(3)
-        gather_words(2, 512, 1024)
-        for h0, h1 in ((0, 1152), (1152, 2304)):
-            for s0 in (h0, h0 + 576):
-                gather_scales(s0, s0 + 576)
+        for a, stop in ((0, SLOTS), (1, SLOTS), (2, EARLY)):
+            new_words(a, 0, stop - P)
+            if stop == SLOTS:
+                gather_words(a, 0, SLOTS // 2)
+                gather_words(a, SLOTS // 2, stop - P)
+            else:
+                gather_words(a, 0, stop - P)
+            for c0, c1 in QUANT[a + 1]:
+                quantise(a + 1, c0, c1)
+            new_words(a, stop - P, stop, tag=f"x_f{a + 1}_{LOADS[a + 1][-1][0]}")
+            gather_words(a, stop - P, stop)
+        for h0, h1 in ((0, SLOTS // 2), (SLOTS // 2, SLOTS)):
+            nc.vector.tensor_copy(g_s[:, h0:h1], x_s[:].indirect(offs_t[:, h0 // 16 : h1 // 16]))
             for q in range(4):
                 nc.sync.dma_start(
                     out=m_s[32 * q : 32 * q + 4, h0:h1].bitcast(I32),
                     in_=g_s[32 * q + 12 : 32 * q + 16, h0:h1].bitcast(I32),
                 )
-        g_w2.append(held.tile([P, SLOTS - 1024], U32, name="g_w2b", tag="late", align_bytes=64))
+        new_words(2, EARLY, SLOTS, tag="x_b3_512")
+        new_words(3, 0, SLOTS)
+
         def acc(g):
-            return bank[g % 8][:, (g // 8) * 128 : (g // 8 + 1) * 128]
+            return bank[g % 8][:, (g // 8) * P : (g // 8 + 1) * P]
 
         def multiply(g, a):
             e = g // 2
-            cols = slice(g * 128, (g + 1) * 128)
+            cols = slice(g * P, (g + 1) * P)
             if a < 2:
                 lhsT = w8_t[:, 2 * e + a, :].bitcast(FP8X4)
             else:
@@ -174,44 +200,79 @@ def tile_moe_tk_lin_relu2_kernel(
 
         def activate(g):
             e = g // 2
-            if g == SLOTS // 128 - 1:
-                nc.vector.tensor_scalar(
-                    relu_t[:, g * 128 : (g + 1) * 128], acc(g), b_t[:, e : e + 1], 0.0, ALU.add, ALU.max
-                )
-                return
-            nc.scalar.activation(relu_t[:, g * 128 : (g + 1) * 128], acc(g), ACT.Relu, bias=b_t[:, e : e + 1])
-
-        def square(s0, s1):
-            nc.scalar.activation(y_t[:, s0:s1], relu_t[:, s0:s1], ACT.Square)
-
-        def open_groups(g0, g1):
-            for g in range(g0, min(g1, SLOTS // 128)):
-                multiply(g, 0)
-                multiply(g, 1)
-
-        open_groups(0, 8)
-        for s0, s1 in ((0, 512), (512, 1024), (1024, 1536), (1536, 2048), (2048, 2304)):
-            if s0 >= 1024:
-                gather_words(2, s0, s1)
-            for g in range(s0 // 128, s1 // 128):
-                multiply(g, 2)
-            pieces = ((s0, s1),) if s1 < SLOTS else ((s0, s0 + 128), (s0 + 128, s1))
-            for p0, p1 in pieces:
-                gather_words(3, p0, p1)
-                for g in range(p0 // 128, p1 // 128):
-                    multiply(g, 3)
-                    activate(g)
-            if s1 < SLOTS:
-                square(s0, s1)
+            if g == GROUPS - 1:
+                nc.vector.tensor_scalar(relu_t[:, g * P : (g + 1) * P], acc(g), b_t[:, e : e + 1], 0.0, ALU.add, ALU.max)
             else:
-                nc.vector.tensor_tensor(y_t[:, s0:s1], relu_t[:, s0:s1], relu_t[:, s0:s1], ALU.mult)
-            open_groups(s0 // 128 + 8, s1 // 128 + 8)
+                nc.scalar.activation(relu_t[:, g * P : (g + 1) * P], acc(g), ACT.Relu, bias=b_t[:, e : e + 1])
+
+        def third_pass(s0, s1):
+            if s0 >= EARLY:
+                gather_words(2, s0, s1)
+            for g in range(s0 // P, s1 // P):
+                multiply(g, 2)
+
+        def last_pass(s0, s1):
+            gather_words(3, s0, s1)
+            for g in range(s0 // P, s1 // P):
+                multiply(g, 3)
+                activate(g)
+                if g + 8 < GROUPS:
+                    multiply(g + 8, 0)
+                    multiply(g + 8, 1)
+            for q0 in range(s0, s1, 512):
+                q1 = min(q0 + 512, s1)
+                nc.scalar.activation(y_t[:, q0:q1], relu_t[:, q0:q1], ACT.Square)
+
+        for g in range(8):
+            multiply(g, 0)
+            multiply(g, 1)
+        third_pass(0, 1024)
+        last_pass(0, 1024)
+        third_pass(1024, 1536)
+        last_pass(1024, 1536)
+        third_pass(1536, 2048)
+        last_pass(1536, 1792)
+        last_pass(1792, 2048)
+        third_pass(2048, 2304)
+        last_pass(2048, 2176)
+        last_pass(2176, 2304)
+
+        back = bank[4:8]
+
+        def turned(r, c):
+            if r < 2:
+                return bank[r][:, c * P : (c + 1) * P]
+            return bank[(c + 2) % 4][:, 0:P]
 
         for r in range(3):
-            nc.vector.tensor_tensor(pick[r][:], y_t[:].indirect(pos_t[r][:]), gate_t[:, r, :], ALU.mult)
-        halves = ((0, 512), (512, 768))
-        for c0, c1 in halves:
-            nc.vector.tensor_tensor(sum_t[:, c0:c1], pick[0][:, c0:c1], pick[1][:, c0:c1], ALU.add)
-        for c0, c1 in halves:
-            nc.vector.tensor_tensor(out_t[:, c0:c1], sum_t[:, c0:c1], pick[2][:, c0:c1], ALU.add)
-            nc.sync.dma_start(out=out[:, c0:c1], in_=out_t[:, c0:c1])
+            nc.vector.tensor_copy(pick[r][:], y_t[:].indirect(pos_t[r][:, 0 : TV // 16]))
+            for c in range(TURNED):
+                nc.tensor.transpose(turned(r, c), pick[r][:, c * P : (c + 1) * P], ident[:])
+            for c in range(TURNED):
+                gate_col = gate_cols[:, TURNED * r + c : TURNED * r + c + 1]
+                nc.scalar.activation(scaled[r][:, c, :], turned(r, c), ACT.Copy, scale=gate_col)
+            for c in range(TURNED):
+                nc.tensor.matmul(
+                    back[c][:, 0:P], scaled[r][:, c, :], ident[:], start=(r == 0), stop=(r == 2), is_transpose=True
+                )
+        for c in range(TURNED):
+            nc.scalar.copy(out_a[:, c * P : (c + 1) * P], back[c][:, 0:P])
+        nc.scalar.dma_start(out=out[:, 0:TV], in_=out_a[:])
+
+        def gated(r, c0, c1):
+            nc.vector.tensor_tensor(
+                prod[r][:, c0:c1],
+                y_t[:].indirect(pos_t[r][:, (TV + c0) // 16 : (TV + c1) // 16]),
+                gate_t[:, r, c0:c1],
+                ALU.mult,
+            )
+
+        rest = T - TV
+        gated(0, 0, rest)
+        gated(1, 0, rest)
+        gated(2, 0, rest // 2)
+        nc.vector.tensor_tensor(sum_t[:], prod[0][:], prod[1][:], ALU.add)
+        gated(2, rest // 2, rest)
+        for c0, c1 in ((0, rest // 2), (rest // 2, rest)):
+            nc.vector.tensor_tensor(out_b[:, c0:c1], sum_t[:, c0:c1], prod[2][:, c0:c1], ALU.add)
+        nc.sync.dma_start(out=out[:, TV:T], in_=out_b[:])

@@ -21,7 +21,8 @@ ALU = mybir.AluOpType
 P = 128
 PASSES = 4
 GROUPS = SLOTS // P
-PLANE = (4, 8, 0, 12)
+ORDER = (0, 2, 3, 1)
+PLANE = (4, 0, 12, 8)
 TURNED = 4
 TV = TURNED * P
 THIRDS = ((0, 256), (256, 512), (512, 768))
@@ -29,7 +30,7 @@ WIDE = ((0, 512), (512, 768))
 LOADS = (THIRDS, THIRDS, WIDE, ((0, 768),))
 QUANT = (THIRDS, WIDE, WIDE, WIDE)
 HEAD_V = 160
-EARLY = 1024
+EARLY = 1280
 
 
 def tile_moe_tk_lin_relu2_kernel(
@@ -60,24 +61,21 @@ def tile_moe_tk_lin_relu2_kernel(
         w4_t = held.tile([P, 2 * E, 2 * N], U8, name="w4_t", align_bytes=64)
         ws_t = held.tile([P, 2, 2 * E, N], U8, name="ws_t", align_bytes=64)
         b_t = held.tile([P, E], F32, name="b_t")
-        gate_t = held.tile([P, 3, T - TV], F32, name="gate_t")
-        gate_rows = held.tile([P, P], F32, name="gate_rows")
-        gate_cols = held.tile([P, 3 * TURNED], F32, name="gate_cols")
+        gate_t = held.tile([P, 3, T], F32, name="gate_t")
         ident = held.tile([P, P], F32, name="ident")
         relu_t = held.tile([P, SLOTS], F32, name="relu_t")
         y_t = held.tile([P, SLOTS], F32, name="y_t")
-        pick = [held.tile([P, TV], F32, name=f"pick{r}") for r in range(3)]
-        scaled = [held.tile([P, TURNED, P], F32, name=f"scaled{r}") for r in range(3)]
+        pick = [[held.tile([P, 256], F32, name=f"pick{h}_{r}") for r in range(3)] for h in range(2)]
+        summed = [held.tile([P, 2, P], F32, name=f"summed{h}") for h in range(2)]
         prod = [held.tile([P, T - TV], F32, name=f"prod{r}") for r in range(3)]
         sum_t = held.tile([P, T - TV], F32, name="sum_t")
-        out_a = held.tile([P, TV], F32, name="out_a")
+        out_a = [held.tile([P, 256], F32, name=f"out_a{h}") for h in range(2)]
         out_b = held.tile([P, T - TV], F32, name="out_b")
         warm = held.tile([P, 1], F32, name="warm")
         bank = [psum.tile([P, 512], F32, name=f"bank{i}") for i in range(8)]
 
         nc.gpsimd.memset(x_s[:].bitcast(I32), 0)
         nc.gpsimd.memset(x_w[:, PASSES * T :], 0)
-        nc.gpsimd.memset(gate_rows[:], 0.0)
         make_identity(nc, ident[:])
         nc.gpsimd.memset(m_s[:].bitcast(I32), 0)
         nc.vector.memset(warm[:], 0.0)
@@ -88,7 +86,7 @@ def tile_moe_tk_lin_relu2_kernel(
 
         def load_x(a):
             for c0, c1 in LOADS[a]:
-                nc.sync.dma_start(out=x_f[a, c0][:], in_=xv[a, :, :, c0:c1])
+                nc.sync.dma_start(out=x_f[a, c0][:], in_=xv[ORDER[a], :, :, c0:c1])
 
         def cast(engine, a, c0, c1):
             f0 = max(lo for lo, hi in LOADS[a] if lo <= c0)
@@ -129,10 +127,6 @@ def tile_moe_tk_lin_relu2_kernel(
         nc.sync.dma_start(offs_t[:], offs)
         for a in (1, 2, 3):
             load_x(a)
-        for r in range(3):
-            nc.sync.dma_start(
-                out=gate_rows[TURNED * r : TURNED * (r + 1), :], in_=gate[r, 0, 0:TV].rearrange("(c p) -> c p", p=P)
-            )
         for s, scales in enumerate((w8_scales, w4_scales)):
             for q in range(4):
                 nc.sync.dma_start(
@@ -144,7 +138,7 @@ def tile_moe_tk_lin_relu2_kernel(
         nc.sync.dma_start(out=b_t[:], in_=b)
         for t, src in zip(pos_t, (pos1, pos2, pos3)):
             nc.sync.dma_start(t[:], src)
-        nc.sync.dma_start(out=gate_t[:], in_=gate[:, :, TV:T].rearrange("r p t -> p r t"))
+        nc.sync.dma_start(out=gate_t[:], in_=gate.rearrange("r p t -> p r t"))
 
         for c0, c1 in THIRDS:
             cast("s", 0, c0 + HEAD_V, c1)
@@ -154,16 +148,11 @@ def tile_moe_tk_lin_relu2_kernel(
             for c0, c1 in THIRDS if a == 1 else WIDE:
                 cast("s", a, c0, c1)
 
-        nc.tensor.transpose(bank[7][:, 0:P], gate_rows[:], ident[:])
-        nc.scalar.copy(gate_cols[:], bank[7][:, 0 : 3 * TURNED])
-
         for a, stop in ((0, SLOTS), (1, SLOTS), (2, EARLY)):
             new_words(a, 0, stop - P)
+            gather_words(a, 0, SLOTS // 2)
             if stop == SLOTS:
-                gather_words(a, 0, SLOTS // 2)
                 gather_words(a, SLOTS // 2, stop - P)
-            else:
-                gather_words(a, 0, stop - P)
             for c0, c1 in QUANT[a + 1]:
                 quantise(a + 1, c0, c1)
             new_words(a, stop - P, stop, tag=f"x_f{a + 1}_{LOADS[a + 1][-1][0]}")
@@ -178,101 +167,92 @@ def tile_moe_tk_lin_relu2_kernel(
         new_words(2, EARLY, SLOTS, tag="x_b3_512")
         new_words(3, 0, SLOTS)
 
-        def acc(g):
-            return bank[g % 8][:, (g // 8) * P : (g // 8 + 1) * P]
+        def acc(s0, s1):
+            if s0 < 8 * C:
+                return bank[s0 // C][:, s0 % C : s0 % C + s1 - s0]
+            return bank[(s0 - 8 * C) // P][:, C : C + P]
 
-        def multiply(g, a):
-            e = g // 2
-            cols = slice(g * P, (g + 1) * P)
-            if a < 2:
-                lhsT = w8_t[:, 2 * e + a, :].bitcast(FP8X4)
+        def multiply(a, s0, s1):
+            e, pas = s0 // C, ORDER[a]
+            if pas < 2:
+                lhsT = w8_t[:, 2 * e + pas, :].bitcast(FP8X4)
             else:
-                lhsT = w4_t[:, 2 * e + a - 2, :].bitcast(FP4X4)
+                lhsT = w4_t[:, 2 * e + pas - 2, :].bitcast(FP4X4)
             nc.tensor.matmul_mx(
-                out=acc(g),
+                out=acc(s0, s1),
                 lhsT=lhsT,
-                lhsT_scale=ws_t[:, a // 2, 2 * e + a % 2, :],
-                rhs=words(a, cols.start, cols.stop).bitcast(FP8X4),
-                rhs_scale=m_s[:, cols] if a == 3 else g_s[PLANE[a] : P, cols],
+                lhsT_scale=ws_t[:, pas // 2, 2 * e + pas % 2, :],
+                rhs=words(a, s0, s1).bitcast(FP8X4),
+                rhs_scale=m_s[:, s0:s1] if a == 2 else g_s[PLANE[a] : P, s0:s1],
                 start=(a == 0),
                 stop=(a == PASSES - 1),
             )
 
-        def activate(g):
-            e = g // 2
-            if g == GROUPS - 1:
-                nc.vector.tensor_scalar(relu_t[:, g * P : (g + 1) * P], acc(g), b_t[:, e : e + 1], 0.0, ALU.add, ALU.max)
-            else:
-                nc.scalar.activation(relu_t[:, g * P : (g + 1) * P], acc(g), ACT.Relu, bias=b_t[:, e : e + 1])
+        def narrow(a, s0, s1):
+            for g0 in range(s0, s1, P):
+                multiply(a, g0, g0 + P)
 
-        def third_pass(s0, s1):
-            if s0 >= EARLY:
-                gather_words(2, s0, s1)
-            for g in range(s0 // P, s1 // P):
-                multiply(g, 2)
+        def third_step(s0, s1):
+            gather_words(2, s0, s1)
+            narrow(2, s0, s1)
 
-        def last_pass(s0, s1):
+        def last_step(s0, s1):
             gather_words(3, s0, s1)
-            for g in range(s0 // P, s1 // P):
-                multiply(g, 3)
-                activate(g)
-                if g + 8 < GROUPS:
-                    multiply(g + 8, 0)
-                    multiply(g + 8, 1)
+            width = min(C, s1 - s0)
+            for g0 in range(s0, s1, width):
+                cols, bias = slice(g0, g0 + width), b_t[:, g0 // C : g0 // C + 1]
+                multiply(3, g0, g0 + width)
+                if g0 >= 8 * C:
+                    nc.vector.tensor_scalar(relu_t[:, cols], acc(g0, g0 + width), bias, 0.0, ALU.add, ALU.max)
+                else:
+                    nc.scalar.activation(relu_t[:, cols], acc(g0, g0 + width), ACT.Relu, bias=bias)
             for q0 in range(s0, s1, 512):
                 q1 = min(q0 + 512, s1)
                 nc.scalar.activation(y_t[:, q0:q1], relu_t[:, q0:q1], ACT.Square)
 
-        for g in range(8):
-            multiply(g, 0)
-            multiply(g, 1)
-        third_pass(0, 1024)
-        last_pass(0, 1024)
-        third_pass(1024, 1536)
-        last_pass(1024, 1536)
-        third_pass(1536, 2048)
-        last_pass(1536, 1792)
-        last_pass(1792, 2048)
-        third_pass(2048, 2304)
-        last_pass(2048, 2176)
-        last_pass(2176, 2304)
+        for e in range(8):
+            multiply(0, e * C, (e + 1) * C)
+            narrow(1, e * C, (e + 1) * C)
+        narrow(2, 0, EARLY)
+        last_step(0, 1024)
+        narrow(0, 8 * C, SLOTS)
+        narrow(1, 8 * C, SLOTS)
+        third_step(EARLY, 1536)
+        last_step(1024, 1536)
+        third_step(1536, 2048)
+        last_step(1536, 1792)
+        last_step(1792, 2048)
+        third_step(2048, 2304)
+        last_step(2048, 2176)
+        last_step(2176, 2304)
 
-        back = bank[4:8]
+        def gated(dst, r, c0, c1):
+            nc.vector.tensor_tensor(dst, y_t[:].indirect(pos_t[r][:, c0 // 16 : c1 // 16]), gate_t[:, r, c0:c1], ALU.mult)
 
-        def turned(r, c):
-            if r < 2:
-                return bank[r][:, c * P : (c + 1) * P]
-            return bank[(c + 2) % 4][:, 0:P]
-
-        for r in range(3):
-            nc.vector.tensor_copy(pick[r][:], y_t[:].indirect(pos_t[r][:, 0 : TV // 16]))
-            for c in range(TURNED):
-                nc.tensor.transpose(turned(r, c), pick[r][:, c * P : (c + 1) * P], ident[:])
-            for c in range(TURNED):
-                gate_col = gate_cols[:, TURNED * r + c : TURNED * r + c + 1]
-                nc.scalar.activation(scaled[r][:, c, :], turned(r, c), ACT.Copy, scale=gate_col)
-            for c in range(TURNED):
-                nc.tensor.matmul(
-                    back[c][:, 0:P], scaled[r][:, c, :], ident[:], start=(r == 0), stop=(r == 2), is_transpose=True
-                )
-        for c in range(TURNED):
-            nc.scalar.copy(out_a[:, c * P : (c + 1) * P], back[c][:, 0:P])
-        nc.scalar.dma_start(out=out[:, 0:TV], in_=out_a[:])
-
-        def gated(r, c0, c1):
-            nc.vector.tensor_tensor(
-                prod[r][:, c0:c1],
-                y_t[:].indirect(pos_t[r][:, (TV + c0) // 16 : (TV + c1) // 16]),
-                gate_t[:, r, c0:c1],
-                ALU.mult,
-            )
+        for h in range(2):
+            for r in range(3):
+                gated(pick[h][r][:], r, 256 * h, 256 * (h + 1))
+                for c in range(2):
+                    nc.tensor.matmul(
+                        bank[2 * h + c][:, 0:P],
+                        pick[h][r][:, c * P : (c + 1) * P],
+                        ident[:],
+                        start=(r == 0),
+                        stop=(r == 2),
+                        is_transpose=True,
+                    )
+            for c in range(2):
+                nc.scalar.copy(summed[h][:, c, :], bank[2 * h + c][:, 0:P])
+                nc.tensor.transpose(bank[4 + h][:, c * P : (c + 1) * P], summed[h][:, c, :], ident[:])
+            nc.scalar.copy(out_a[h][:], bank[4 + h][:, 0:256])
+            nc.scalar.dma_start(out=out[:, 256 * h : 256 * (h + 1)], in_=out_a[h][:])
 
         rest = T - TV
-        gated(0, 0, rest)
-        gated(1, 0, rest)
-        gated(2, 0, rest // 2)
+        gated(prod[0][:], 0, TV, T)
+        gated(prod[1][:], 1, TV, T)
+        gated(prod[2][:, 0 : rest // 2], 2, TV, TV + rest // 2)
         nc.vector.tensor_tensor(sum_t[:], prod[0][:], prod[1][:], ALU.add)
-        gated(2, rest // 2, rest)
+        gated(prod[2][:, rest // 2 :], 2, TV + rest // 2, T)
         for c0, c1 in ((0, rest // 2), (rest // 2, rest)):
             nc.vector.tensor_tensor(out_b[:, c0:c1], sum_t[:, c0:c1], prod[2][:, c0:c1], ALU.add)
         nc.sync.dma_start(out=out[:, TV:T], in_=out_b[:])

@@ -23,13 +23,14 @@ PASSES = 4
 GROUPS = SLOTS // P
 ORDER = (0, 2, 3, 1)
 PLANE = (4, 0, 12, 8)
+W8_PLANE = 8
 TURNED = 4
 TV = TURNED * P
 THIRDS = ((0, 256), (256, 512), (512, 768))
 WIDE = ((0, 512), (512, 768))
-LOADS = (THIRDS, THIRDS, WIDE, ((0, 768),))
-QUANT = (THIRDS, WIDE, WIDE, WIDE)
-HEAD_V = 160
+HEAD = ((0, 256), (256, 512), (512, 640), (640, 768))
+LOADS = (HEAD, THIRDS, WIDE, ((0, 768),))
+QUANT = (HEAD, WIDE, WIDE, WIDE)
 EARLY = 1280
 
 
@@ -59,7 +60,7 @@ def tile_moe_tk_lin_relu2_kernel(
         m_s = held.tile([P, SLOTS], U8, name="m_s", align_bytes=64)
         w8_t = held.tile([P, 2 * E, 4 * N], U8, name="w8_t", align_bytes=64)
         w4_t = held.tile([P, 2 * E, 2 * N], U8, name="w4_t", align_bytes=64)
-        ws_t = held.tile([P, 2, 2 * E, N], U8, name="ws_t", align_bytes=64)
+        ws_t = held.tile([P, 2 * E, N], U8, name="ws_t", align_bytes=64)
         b_t = held.tile([P, E], F32, name="b_t")
         gate_t = held.tile([P, 3, T], F32, name="gate_t")
         ident = held.tile([P, P], F32, name="ident")
@@ -74,12 +75,12 @@ def tile_moe_tk_lin_relu2_kernel(
         warm = held.tile([P, 1], F32, name="warm")
         bank = [psum.tile([P, 512], F32, name=f"bank{i}") for i in range(8)]
 
-        nc.gpsimd.memset(x_s[:].bitcast(I32), 0)
-        nc.gpsimd.memset(x_w[:, PASSES * T :], 0)
-        make_identity(nc, ident[:])
         nc.gpsimd.memset(m_s[:].bitcast(I32), 0)
+        make_identity(nc, ident[:])
         nc.vector.memset(warm[:], 0.0)
-        nc.vector.memset(ws_t[:].rearrange("p s g n -> p (s g n)").bitcast(I32), 0)
+        nc.vector.memset(x_s[:].bitcast(I32), 0)
+        nc.vector.memset(x_w[:, PASSES * T :], 0)
+        nc.vector.memset(ws_t[:].rearrange("p g n -> p (g n)").bitcast(I32), 0)
         nc.scalar.activation(warm[:], warm[:], ACT.Square)
 
         xv = xT.rearrange("(a p j) t -> a p j t", a=PASSES, j=4)
@@ -127,10 +128,10 @@ def tile_moe_tk_lin_relu2_kernel(
         nc.sync.dma_start(offs_t[:], offs)
         for a in (1, 2, 3):
             load_x(a)
-        for s, scales in enumerate((w8_scales, w4_scales)):
+        for row, scales in ((W8_PLANE, w8_scales), (0, w4_scales)):
             for q in range(4):
                 nc.sync.dma_start(
-                    out=ws_t[32 * q : 32 * q + 4, s].bitcast(I32),
+                    out=ws_t[32 * q + row : 32 * q + row + 4].bitcast(I32),
                     in_=scales[:, :, 4 * q : 4 * q + 4, :].rearrange("e a q n -> q (e a) n").bitcast(I32),
                 )
         nc.sync.dma_start(out=w8_t[:].bitcast(I32), in_=w8_words.rearrange("e a p n r -> p (e a) (n r)").bitcast(I32))
@@ -140,9 +141,10 @@ def tile_moe_tk_lin_relu2_kernel(
             nc.sync.dma_start(t[:], src)
         nc.sync.dma_start(out=gate_t[:], in_=gate.rearrange("r p t -> p r t"))
 
-        for c0, c1 in THIRDS:
-            cast("s", 0, c0 + HEAD_V, c1)
-            cast("v", 0, c0, c0 + HEAD_V)
+        for c0, c1 in HEAD:
+            cut = c0 + (c1 - c0) * 5 // 8
+            cast("s", 0, cut, c1)
+            cast("v", 0, c0, cut)
             quantise(0, c0, c1)
         for a in (1, 2, 3):
             for c0, c1 in THIRDS if a == 1 else WIDE:
@@ -181,7 +183,7 @@ def tile_moe_tk_lin_relu2_kernel(
             nc.tensor.matmul_mx(
                 out=acc(s0, s1),
                 lhsT=lhsT,
-                lhsT_scale=ws_t[:, pas // 2, 2 * e + pas % 2, :],
+                lhsT_scale=ws_t[(W8_PLANE if pas < 2 else 0) : P, 2 * e + pas % 2, :],
                 rhs=words(a, s0, s1).bitcast(FP8X4),
                 rhs_scale=m_s[:, s0:s1] if a == 2 else g_s[PLANE[a] : P, s0:s1],
                 start=(a == 0),
@@ -255,4 +257,4 @@ def tile_moe_tk_lin_relu2_kernel(
         gated(prod[2][:, rest // 2 :], 2, TV + rest // 2, T)
         for c0, c1 in ((0, rest // 2), (rest // 2, rest)):
             nc.vector.tensor_tensor(out_b[:, c0:c1], sum_t[:, c0:c1], prod[2][:, c0:c1], ALU.add)
-        nc.sync.dma_start(out=out[:, TV:T], in_=out_b[:])
+            nc.sync.dma_start(out=out[:, TV + c0 : TV + c1], in_=out_b[:, c0:c1])

@@ -19,19 +19,34 @@ ACT = mybir.ActivationFunctionType
 ALU = mybir.AluOpType
 
 P = 128
-PASSES = 4
-GROUPS = SLOTS // P
+TOP = 3
+STEPS = 4
+BANKS = 8
+QUADRANTS = 4
+
 ORDER = (0, 2, 3, 1)
 PLANE = (4, 0, 12, 8)
+MOVED = 2
 W8_PLANE = 8
-TURNED = 4
-TV = TURNED * P
+
+HEAD = ((0, 256), (256, 512), (512, 640), (640, 768))
 THIRDS = ((0, 256), (256, 512), (512, 768))
 WIDE = ((0, 512), (512, 768))
-HEAD = ((0, 256), (256, 512), (512, 640), (640, 768))
-LOADS = (HEAD, THIRDS, WIDE, ((0, 768),))
+LOADS = (HEAD, THIRDS, WIDE, ((0, T),))
+ROUNDS = (HEAD, THIRDS, WIDE, WIDE)
 QUANT = (HEAD, WIDE, WIDE, WIDE)
-EARLY = 1280
+HEAD_EIGHTHS = 5
+
+HALF = SLOTS // 2
+SHORT = 3 * T // 4
+EARLY = HALF + P
+LAST = BANKS * C
+SQUARE = 512
+
+STRETCH = 256
+STRETCHES = 2
+TURNED = STRETCHES * STRETCH
+REST = T - TURNED
 
 
 def tile_moe_tk_lin_relu2_kernel(
@@ -43,218 +58,214 @@ def tile_moe_tk_lin_relu2_kernel(
         psum = ctx.enter_context(tc.psum_pool(name="psum", bufs=1))
 
         offs_t = held.tile([P, SLOTS // 16], U16, name="offs_t")
-        pos_t = [held.tile([P, T // 16], U16, name=f"pos_t{r}") for r in range(3)]
+        pos_t = [held.tile([P, T // 16], U16, name=f"pos_t{r}") for r in range(TOP)]
         x_f = {
-            (a, c0): held.tile([P, 4, c1 - c0], F32, name=f"x_f{a}_{c0}", align_bytes=64)
-            for a in range(PASSES)
-            for c0, c1 in LOADS[a]
+            (step, t0): held.tile([P, 4, t1 - t0], F32, name=f"x_f{step}_{t0}", align_bytes=64)
+            for step in range(STEPS)
+            for t0, t1 in LOADS[step]
         }
         x_b = {
-            (a, c0): held.tile([P, c1 - c0, 4], BF16, name=f"x_b{a}_{c0}", align_bytes=64)
-            for a in range(PASSES)
-            for c0, c1 in QUANT[a]
+            (step, t0): held.tile([P, t1 - t0, 4], BF16, name=f"x_b{step}_{t0}", align_bytes=64)
+            for step in range(STEPS)
+            for t0, t1 in QUANT[step]
         }
-        x_w = held.tile([P, (PASSES + 1) * T], I32, name="x_w", align_bytes=64)
-        x_s = held.tile([P, 2 * T], U8, name="x_s", align_bytes=64)
-        g_s = held.tile([P, SLOTS], U8, name="g_s", align_bytes=64)
-        m_s = held.tile([P, SLOTS], U8, name="m_s", align_bytes=64)
+        x_words = held.tile([P, (STEPS + 1) * T], I32, name="x_words", align_bytes=64)
+        x_scales = held.tile([P, 2 * T], U8, name="x_scales", align_bytes=64)
+        slot_scales = held.tile([P, SLOTS], U8, name="slot_scales", align_bytes=64)
+        moved_scales = held.tile([P, SLOTS], U8, name="moved_scales", align_bytes=64)
         w8_t = held.tile([P, 2 * E, 4 * N], U8, name="w8_t", align_bytes=64)
         w4_t = held.tile([P, 2 * E, 2 * N], U8, name="w4_t", align_bytes=64)
-        ws_t = held.tile([P, 2 * E, N], U8, name="ws_t", align_bytes=64)
+        w_scales = held.tile([P, 2 * E, N], U8, name="w_scales", align_bytes=64)
         b_t = held.tile([P, E], F32, name="b_t")
-        gate_t = held.tile([P, 3, T], F32, name="gate_t")
+        gate_t = held.tile([P, TOP, T], F32, name="gate_t")
         ident = held.tile([P, P], F32, name="ident")
         relu_t = held.tile([P, SLOTS], F32, name="relu_t")
         y_t = held.tile([P, SLOTS], F32, name="y_t")
-        pick = [[held.tile([P, 256], F32, name=f"pick{h}_{r}") for r in range(3)] for h in range(2)]
-        summed = [held.tile([P, 2, P], F32, name=f"summed{h}") for h in range(2)]
-        prod = [held.tile([P, T - TV], F32, name=f"prod{r}") for r in range(3)]
-        sum_t = held.tile([P, T - TV], F32, name="sum_t")
-        out_a = [held.tile([P, 256], F32, name=f"out_a{h}") for h in range(2)]
-        out_b = held.tile([P, T - TV], F32, name="out_b")
-        warm = held.tile([P, 1], F32, name="warm")
-        bank = [psum.tile([P, 512], F32, name=f"bank{i}") for i in range(8)]
+        gated_t = [[held.tile([P, STRETCH], F32, name=f"gated{h}_{r}") for r in range(TOP)] for h in range(STRETCHES)]
+        summed = [held.tile([P, STRETCH // P, P], F32, name=f"summed{h}") for h in range(STRETCHES)]
+        rest_gated = [held.tile([P, REST], F32, name=f"rest_gated{r}") for r in range(TOP)]
+        rest_pair = held.tile([P, REST], F32, name="rest_pair")
+        out_turned = [held.tile([P, STRETCH], F32, name=f"out_turned{h}") for h in range(STRETCHES)]
+        out_rest = held.tile([P, REST], F32, name="out_rest")
+        bank = [psum.tile([P, 512], F32, name=f"bank{i}") for i in range(BANKS)]
 
-        nc.gpsimd.memset(m_s[:].bitcast(I32), 0)
+        nc.gpsimd.memset(moved_scales[:].bitcast(I32), 0)
         make_identity(nc, ident[:])
-        nc.vector.memset(warm[:], 0.0)
-        nc.vector.memset(x_s[:].bitcast(I32), 0)
-        nc.vector.memset(x_w[:, PASSES * T :], 0)
-        nc.vector.memset(ws_t[:].rearrange("p g n -> p (g n)").bitcast(I32), 0)
-        nc.scalar.activation(warm[:], warm[:], ACT.Square)
+        nc.vector.memset(x_scales[:].bitcast(I32), 0)
+        nc.vector.memset(x_words[:, STEPS * T :], 0)
+        nc.vector.memset(w_scales[:].rearrange("p g n -> p (g n)").bitcast(I32), 0)
 
-        xv = xT.rearrange("(a p j) t -> a p j t", a=PASSES, j=4)
+        x_rows = xT.rearrange("(a p j) t -> a p j t", a=STEPS, j=4)
 
-        def load_x(a):
-            for c0, c1 in LOADS[a]:
-                nc.sync.dma_start(out=x_f[a, c0][:], in_=xv[ORDER[a], :, :, c0:c1])
-
-        def cast(engine, a, c0, c1):
-            f0 = max(lo for lo, hi in LOADS[a] if lo <= c0)
-            b0 = max(lo for lo, hi in QUANT[a] if lo <= c0)
-            src = x_f[a, f0][:, :, c0 - f0 : c1 - f0].rearrange("p j (c i) -> p c j i", i=4)
-            dst = x_b[a, b0][:, c0 - b0 : c1 - b0, :].rearrange("p (c i) j -> p c j i", i=4)
-            if engine == "v":
-                nc.vector.tensor_copy(dst, src)
-            else:
-                nc.scalar.activation(dst, src, ACT.Copy)
-
-        def first_word(a):
-            return (PASSES - 1 - a) * T
-
-        def quantise(a, c0, c1):
-            nc.vector.quantize_mx(
-                out=x_w[:, first_word(a) + c0 : first_word(a) + c1].bitcast(FP8X4),
-                scales=x_s[PLANE[a] : P, c0:c1],
-                in_=x_b[a, c0][:].rearrange("p t j -> p (t j)"),
-            )
-
-        g_w = {}
-
-        def new_words(a, s0, s1, tag=None):
-            name = f"g_w{a}_{s0}"
-            g_w[a, s0] = held.tile([P, s1 - s0], U32, name=name, tag=tag or name, align_bytes=64)
-
-        def words(a, s0, s1):
-            lo = max(first for pas, first in g_w if pas == a and first <= s0)
-            return g_w[a, lo][:, s0 - lo : s1 - lo]
-
-        def gather_words(a, s0, s1):
-            width = T if s1 - s0 <= 576 else 2 * T
-            window = x_w[:, first_word(a) : first_word(a) + width].bitcast(U32)
-            nc.vector.tensor_copy(words(a, s0, s1), window.indirect(offs_t[:, s0 // 16 : s1 // 16]))
+        def load_x(step):
+            for t0, t1 in LOADS[step]:
+                nc.sync.dma_start(out=x_f[step, t0][:], in_=x_rows[ORDER[step], :, :, t0:t1])
 
         load_x(0)
         nc.sync.dma_start(offs_t[:], offs)
-        for a in (1, 2, 3):
-            load_x(a)
-        for row, scales in ((W8_PLANE, w8_scales), (0, w4_scales)):
-            for q in range(4):
+        for step in range(1, STEPS):
+            load_x(step)
+        for first, scales in ((W8_PLANE, w8_scales), (0, w4_scales)):
+            for q in range(QUADRANTS):
                 nc.sync.dma_start(
-                    out=ws_t[32 * q + row : 32 * q + row + 4].bitcast(I32),
+                    out=w_scales[32 * q + first : 32 * q + first + 4].bitcast(I32),
                     in_=scales[:, :, 4 * q : 4 * q + 4, :].rearrange("e a q n -> q (e a) n").bitcast(I32),
                 )
         nc.sync.dma_start(out=w8_t[:].bitcast(I32), in_=w8_words.rearrange("e a p n r -> p (e a) (n r)").bitcast(I32))
         nc.sync.dma_start(out=w4_t[:].bitcast(I32), in_=w4_words.rearrange("e a p n -> p (e a) n").bitcast(I32))
         nc.sync.dma_start(out=b_t[:], in_=b)
-        for t, src in zip(pos_t, (pos1, pos2, pos3)):
-            nc.sync.dma_start(t[:], src)
+        for pos_tile, pos in zip(pos_t, (pos1, pos2, pos3)):
+            nc.sync.dma_start(pos_tile[:], pos)
         nc.sync.dma_start(out=gate_t[:], in_=gate.rearrange("r p t -> p r t"))
 
-        for c0, c1 in HEAD:
-            cut = c0 + (c1 - c0) * 5 // 8
-            cast("s", 0, cut, c1)
-            cast("v", 0, c0, cut)
-            quantise(0, c0, c1)
-        for a in (1, 2, 3):
-            for c0, c1 in THIRDS if a == 1 else WIDE:
-                cast("s", a, c0, c1)
+        def round_views(step, t0, t1):
+            f0 = max(lo for lo, hi in LOADS[step] if lo <= t0)
+            b0 = max(lo for lo, hi in QUANT[step] if lo <= t0)
+            src = x_f[step, f0][:, :, t0 - f0 : t1 - f0].rearrange("p j (c i) -> p c j i", i=4)
+            dst = x_b[step, b0][:, t0 - b0 : t1 - b0, :].rearrange("p (c i) j -> p c j i", i=4)
+            return dst, src
 
-        for a, stop in ((0, SLOTS), (1, SLOTS), (2, EARLY)):
-            new_words(a, 0, stop - P)
-            gather_words(a, 0, SLOTS // 2)
-            if stop == SLOTS:
-                gather_words(a, SLOTS // 2, stop - P)
-            for c0, c1 in QUANT[a + 1]:
-                quantise(a + 1, c0, c1)
-            new_words(a, stop - P, stop, tag=f"x_f{a + 1}_{LOADS[a + 1][-1][0]}")
-            gather_words(a, stop - P, stop)
-        for h0, h1 in ((0, SLOTS // 2), (SLOTS // 2, SLOTS)):
-            nc.vector.tensor_copy(g_s[:, h0:h1], x_s[:].indirect(offs_t[:, h0 // 16 : h1 // 16]))
-            for q in range(4):
-                nc.sync.dma_start(
-                    out=m_s[32 * q : 32 * q + 4, h0:h1].bitcast(I32),
-                    in_=g_s[32 * q + 12 : 32 * q + 16, h0:h1].bitcast(I32),
-                )
-        new_words(2, EARLY, SLOTS, tag="x_b3_512")
-        new_words(3, 0, SLOTS)
+        def first_word(step):
+            return (STEPS - 1 - step) * T
 
-        def acc(s0, s1):
-            if s0 < 8 * C:
-                return bank[s0 // C][:, s0 % C : s0 % C + s1 - s0]
-            return bank[(s0 - 8 * C) // P][:, C : C + P]
-
-        def multiply(a, s0, s1):
-            e, pas = s0 // C, ORDER[a]
-            if pas < 2:
-                lhsT = w8_t[:, 2 * e + pas, :].bitcast(FP8X4)
-            else:
-                lhsT = w4_t[:, 2 * e + pas - 2, :].bitcast(FP4X4)
-            nc.tensor.matmul_mx(
-                out=acc(s0, s1),
-                lhsT=lhsT,
-                lhsT_scale=ws_t[(W8_PLANE if pas < 2 else 0) : P, 2 * e + pas % 2, :],
-                rhs=words(a, s0, s1).bitcast(FP8X4),
-                rhs_scale=m_s[:, s0:s1] if a == 2 else g_s[PLANE[a] : P, s0:s1],
-                start=(a == 0),
-                stop=(a == PASSES - 1),
+        def quantise(step, t0, t1):
+            nc.vector.quantize_mx(
+                out=x_words[:, first_word(step) + t0 : first_word(step) + t1].bitcast(FP8X4),
+                scales=x_scales[PLANE[step] : P, t0:t1],
+                in_=x_b[step, t0][:].rearrange("p t j -> p (t j)"),
             )
 
-        def narrow(a, s0, s1):
+        slot_words = {}
+
+        def new_words(step, s0, s1, tag=None):
+            name = f"slot_words{step}_{s0}"
+            slot_words[step, s0] = held.tile([P, s1 - s0], U32, name=name, tag=tag or name, align_bytes=64)
+
+        def words(step, s0, s1):
+            lo = max(first for of_step, first in slot_words if of_step == step and first <= s0)
+            return slot_words[step, lo][:, s0 - lo : s1 - lo]
+
+        def gather_words(step, s0, s1):
+            width = T if s1 - s0 <= SHORT else 2 * T
+            window = x_words[:, first_word(step) : first_word(step) + width].bitcast(U32)
+            nc.vector.tensor_copy(words(step, s0, s1), window.indirect(offs_t[:, s0 // 16 : s1 // 16]))
+
+        for t0, t1 in ROUNDS[0]:
+            cut = t0 + (t1 - t0) * HEAD_EIGHTHS // 8
+            nc.scalar.activation(*round_views(0, cut, t1), ACT.Copy)
+            nc.vector.tensor_copy(*round_views(0, t0, cut))
+            quantise(0, t0, t1)
+        for step in range(1, STEPS):
+            for t0, t1 in ROUNDS[step]:
+                nc.scalar.activation(*round_views(step, t0, t1), ACT.Copy)
+
+        for step, stop in ((0, SLOTS), (1, SLOTS), (2, EARLY)):
+            new_words(step, 0, stop - P)
+            for s0 in range(0, stop - P, HALF):
+                gather_words(step, s0, min(s0 + HALF, stop - P))
+            for t0, t1 in QUANT[step + 1]:
+                quantise(step + 1, t0, t1)
+            new_words(step, stop - P, stop, tag=f"x_f{step + 1}_{LOADS[step + 1][-1][0]}")
+            gather_words(step, stop - P, stop)
+
+        for s0 in range(0, SLOTS, HALF):
+            s1 = s0 + HALF
+            nc.vector.tensor_copy(slot_scales[:, s0:s1], x_scales[:].indirect(offs_t[:, s0 // 16 : s1 // 16]))
+            for q in range(QUADRANTS):
+                row = 32 * q + PLANE[MOVED]
+                nc.sync.dma_start(
+                    out=moved_scales[32 * q : 32 * q + 4, s0:s1].bitcast(I32),
+                    in_=slot_scales[row : row + 4, s0:s1].bitcast(I32),
+                )
+        new_words(2, EARLY, SLOTS, tag=f"x_b3_{QUANT[3][-1][0]}")
+        new_words(3, 0, SLOTS)
+
+        def sums(s0, s1):
+            if s0 < LAST:
+                return bank[s0 // C][:, s0 % C : s0 % C + s1 - s0]
+            return bank[(s0 - LAST) // P][:, C : C + P]
+
+        def multiply(step, s0, s1):
+            matrix = 2 * (s0 // C) + ORDER[step] % 2
+            is_fp8 = ORDER[step] < 2
+            nc.tensor.matmul_mx(
+                out=sums(s0, s1),
+                lhsT=w8_t[:, matrix, :].bitcast(FP8X4) if is_fp8 else w4_t[:, matrix, :].bitcast(FP4X4),
+                lhsT_scale=w_scales[(W8_PLANE if is_fp8 else 0) : P, matrix, :],
+                rhs=words(step, s0, s1).bitcast(FP8X4),
+                rhs_scale=moved_scales[:, s0:s1] if step == MOVED else slot_scales[PLANE[step] : P, s0:s1],
+                start=(step == 0),
+                stop=(step == STEPS - 1),
+            )
+
+        def multiply_narrow(step, s0, s1):
             for g0 in range(s0, s1, P):
-                multiply(a, g0, g0 + P)
+                multiply(step, g0, g0 + P)
 
-        def third_step(s0, s1):
+        def step_2(s0, s1):
             gather_words(2, s0, s1)
-            narrow(2, s0, s1)
+            multiply_narrow(2, s0, s1)
 
-        def last_step(s0, s1):
+        def step_3(s0, s1):
             gather_words(3, s0, s1)
             width = min(C, s1 - s0)
             for g0 in range(s0, s1, width):
                 cols, bias = slice(g0, g0 + width), b_t[:, g0 // C : g0 // C + 1]
                 multiply(3, g0, g0 + width)
-                if g0 >= 8 * C:
-                    nc.vector.tensor_scalar(relu_t[:, cols], acc(g0, g0 + width), bias, 0.0, ALU.add, ALU.max)
+                if g0 >= LAST:
+                    nc.vector.tensor_scalar(relu_t[:, cols], sums(g0, g0 + width), bias, 0.0, ALU.add, ALU.max)
                 else:
-                    nc.scalar.activation(relu_t[:, cols], acc(g0, g0 + width), ACT.Relu, bias=bias)
-            for q0 in range(s0, s1, 512):
-                q1 = min(q0 + 512, s1)
+                    nc.scalar.activation(relu_t[:, cols], sums(g0, g0 + width), ACT.Relu, bias=bias)
+            for q0 in range(s0, s1, SQUARE):
+                q1 = min(q0 + SQUARE, s1)
                 nc.scalar.activation(y_t[:, q0:q1], relu_t[:, q0:q1], ACT.Square)
 
-        for e in range(8):
+        for e in range(BANKS):
             multiply(0, e * C, (e + 1) * C)
-            narrow(1, e * C, (e + 1) * C)
-        narrow(2, 0, EARLY)
-        last_step(0, 1024)
-        narrow(0, 8 * C, SLOTS)
-        narrow(1, 8 * C, SLOTS)
-        third_step(EARLY, 1536)
-        last_step(1024, 1536)
-        third_step(1536, 2048)
-        last_step(1536, 1792)
-        last_step(1792, 2048)
-        third_step(2048, 2304)
-        last_step(2048, 2176)
-        last_step(2176, 2304)
+            multiply_narrow(1, e * C, (e + 1) * C)
+        multiply_narrow(2, 0, EARLY)
+        step_3(0, 4 * C)
+        multiply_narrow(0, LAST, SLOTS)
+        multiply_narrow(1, LAST, SLOTS)
+        step_2(EARLY, 6 * C)
+        step_3(4 * C, 6 * C)
+        step_2(6 * C, LAST)
+        step_3(6 * C, 7 * C)
+        step_3(7 * C, LAST)
+        step_2(LAST, SLOTS)
+        step_3(LAST, LAST + P)
+        step_3(LAST + P, SLOTS)
 
-        def gated(dst, r, c0, c1):
-            nc.vector.tensor_tensor(dst, y_t[:].indirect(pos_t[r][:, c0 // 16 : c1 // 16]), gate_t[:, r, c0:c1], ALU.mult)
+        def gather_gated(dst, r, t0, t1):
+            picked = y_t[:].indirect(pos_t[r][:, t0 // 16 : t1 // 16])
+            nc.vector.tensor_tensor(dst, picked, gate_t[:, r, t0:t1], ALU.mult)
 
-        for h in range(2):
-            for r in range(3):
-                gated(pick[h][r][:], r, 256 * h, 256 * (h + 1))
-                for c in range(2):
+        blocks = STRETCH // P
+        for h in range(STRETCHES):
+            for r in range(TOP):
+                gather_gated(gated_t[h][r][:], r, STRETCH * h, STRETCH * (h + 1))
+                for c in range(blocks):
                     nc.tensor.matmul(
-                        bank[2 * h + c][:, 0:P],
-                        pick[h][r][:, c * P : (c + 1) * P],
+                        bank[blocks * h + c][:, 0:P],
+                        gated_t[h][r][:, c * P : (c + 1) * P],
                         ident[:],
                         start=(r == 0),
-                        stop=(r == 2),
+                        stop=(r == TOP - 1),
                         is_transpose=True,
                     )
-            for c in range(2):
-                nc.scalar.copy(summed[h][:, c, :], bank[2 * h + c][:, 0:P])
-                nc.tensor.transpose(bank[4 + h][:, c * P : (c + 1) * P], summed[h][:, c, :], ident[:])
-            nc.scalar.copy(out_a[h][:], bank[4 + h][:, 0:256])
-            nc.scalar.dma_start(out=out[:, 256 * h : 256 * (h + 1)], in_=out_a[h][:])
+            back = bank[blocks * STRETCHES + h]
+            for c in range(blocks):
+                nc.scalar.copy(summed[h][:, c, :], bank[blocks * h + c][:, 0:P])
+                nc.tensor.transpose(back[:, c * P : (c + 1) * P], summed[h][:, c, :], ident[:])
+            nc.scalar.copy(out_turned[h][:], back[:, 0:STRETCH])
+            nc.scalar.dma_start(out=out[:, STRETCH * h : STRETCH * (h + 1)], in_=out_turned[h][:])
 
-        rest = T - TV
-        gated(prod[0][:], 0, TV, T)
-        gated(prod[1][:], 1, TV, T)
-        gated(prod[2][:, 0 : rest // 2], 2, TV, TV + rest // 2)
-        nc.vector.tensor_tensor(sum_t[:], prod[0][:], prod[1][:], ALU.add)
-        gated(prod[2][:, rest // 2 :], 2, TV + rest // 2, T)
-        for c0, c1 in ((0, rest // 2), (rest // 2, rest)):
-            nc.vector.tensor_tensor(out_b[:, c0:c1], sum_t[:, c0:c1], prod[2][:, c0:c1], ALU.add)
-            nc.sync.dma_start(out=out[:, TV + c0 : TV + c1], in_=out_b[:, c0:c1])
+        mid = REST // 2
+        gather_gated(rest_gated[0][:], 0, TURNED, T)
+        gather_gated(rest_gated[1][:], 1, TURNED, T)
+        gather_gated(rest_gated[2][:, 0:mid], 2, TURNED, TURNED + mid)
+        nc.vector.tensor_tensor(rest_pair[:], rest_gated[0][:], rest_gated[1][:], ALU.add)
+        gather_gated(rest_gated[2][:, mid:], 2, TURNED + mid, T)
+        for c0, c1 in ((0, mid), (mid, REST)):
+            nc.vector.tensor_tensor(out_rest[:, c0:c1], rest_pair[:, c0:c1], rest_gated[2][:, c0:c1], ALU.add)
+            nc.sync.dma_start(out=out[:, TURNED + c0 : TURNED + c1], in_=out_rest[:, c0:c1])

@@ -70,14 +70,13 @@ def tile_moe_tk_lin_relu2_kernel(
             for t0, t1 in QUANT[step]
         }
         x_words = held.tile([P, (STEPS + 1) * T], I32, name="x_words", align_bytes=64)
-        x_scales = held.tile([P, 2 * T], U8, name="x_scales", align_bytes=64)
+        x_scales = held.tile([P, 2 * T], U8, name="x_scales", tag="x_scales", align_bytes=64)
         slot_scales = held.tile([P, SLOTS], U8, name="slot_scales", align_bytes=64)
         moved_scales = held.tile([P, SLOTS], U8, name="moved_scales", align_bytes=64)
         w8_t = held.tile([P, 2 * E, 4 * N], U8, name="w8_t", align_bytes=64)
         w4_t = held.tile([P, 2 * E, 2 * N], U8, name="w4_t", align_bytes=64)
         w_scales = held.tile([P, 2 * E, N], U8, name="w_scales", align_bytes=64)
         b_t = held.tile([P, E], F32, name="b_t")
-        gate_t = held.tile([P, TOP, T], F32, name="gate_t")
         ident = held.tile([P, P], F32, name="ident")
         relu_t = held.tile([P, SLOTS], F32, name="relu_t")
         y_t = held.tile([P, SLOTS], F32, name="y_t")
@@ -116,7 +115,6 @@ def tile_moe_tk_lin_relu2_kernel(
         nc.sync.dma_start(out=b_t[:], in_=b)
         for pos_tile, pos in zip(pos_t, (pos1, pos2, pos3)):
             nc.sync.dma_start(pos_tile[:], pos)
-        nc.sync.dma_start(out=gate_t[:], in_=gate.rearrange("r p t -> p r t"))
 
         def round_views(step, t0, t1):
             f0 = max(lo for lo, hi in LOADS[step] if lo <= t0)
@@ -168,8 +166,7 @@ def tile_moe_tk_lin_relu2_kernel(
             new_words(step, stop - P, stop, tag=f"x_f{step + 1}_{LOADS[step + 1][-1][0]}")
             gather_words(step, stop - P, stop)
 
-        for s0 in range(0, SLOTS, HALF):
-            s1 = s0 + HALF
+        def gather_scales(s0, s1):
             nc.vector.tensor_copy(slot_scales[:, s0:s1], x_scales[:].indirect(offs_t[:, s0 // 16 : s1 // 16]))
             for q in range(QUADRANTS):
                 row = 32 * q + PLANE[MOVED]
@@ -182,8 +179,8 @@ def tile_moe_tk_lin_relu2_kernel(
 
         def sums(s0, s1):
             if s0 < LAST:
-                return bank[s0 // C][:, s0 % C : s0 % C + s1 - s0]
-            return bank[(s0 - LAST) // P][:, C : C + P]
+                return bank[s0 // C % 4][:, s0 // (4 * C) * C + s0 % C :][:, 0 : s1 - s0]
+            return bank[(s0 - LAST) // P][:, 0:P]
 
         def multiply(step, s0, s1):
             matrix = 2 * (s0 // C) + ORDER[step] % 2
@@ -220,16 +217,26 @@ def tile_moe_tk_lin_relu2_kernel(
                 q1 = min(q0 + SQUARE, s1)
                 nc.scalar.activation(y_t[:, q0:q1], relu_t[:, q0:q1], ACT.Square)
 
-        for e in range(BANKS):
-            multiply(0, e * C, (e + 1) * C)
-            multiply_narrow(1, e * C, (e + 1) * C)
-        multiply_narrow(2, 0, EARLY)
-        step_3(0, 4 * C)
+        def open_sums(e0, e1):
+            for e in range(e0, e1):
+                multiply(0, e * C, (e + 1) * C)
+                multiply_narrow(1, e * C, (e + 1) * C)
+
+        gather_scales(0, HALF)
+        open_sums(0, 4)
+        multiply_narrow(2, 0, 4 * C)
+        gather_scales(HALF, SLOTS)
+        step_3(0, 2 * C)
+        gate_t = held.tile([P, TOP, T], F32, name="gate_t", tag="x_scales", align_bytes=64)
+        nc.sync.dma_start(out=gate_t[:], in_=gate.rearrange("r p t -> p r t"))
+        open_sums(4, 6)
+        multiply_narrow(2, 4 * C, EARLY)
+        step_3(2 * C, 5 * C)
+        open_sums(6, 8)
+        step_2(EARLY, LAST)
+        step_3(5 * C, 6 * C)
         multiply_narrow(0, LAST, SLOTS)
         multiply_narrow(1, LAST, SLOTS)
-        step_2(EARLY, 6 * C)
-        step_3(4 * C, 6 * C)
-        step_2(6 * C, LAST)
         step_3(6 * C, 7 * C)
         step_3(7 * C, LAST)
         step_2(LAST, SLOTS)

@@ -35,7 +35,7 @@ WIDE = ((0, 512), (512, 768))
 LOADS = (HEAD, THIRDS, WIDE, ((0, T),))
 ROUNDS = (HEAD, THIRDS, WIDE, WIDE)
 QUANT = (HEAD, WIDE, WIDE, WIDE)
-HEAD_EIGHTHS = 5
+HEAD_EIGHTHS = (5, 5, 5, 5)
 
 HALF = SLOTS // 2
 SHORT = 3 * T // 4
@@ -69,8 +69,8 @@ def tile_moe_tk_lin_relu2_kernel(
             for step in range(STEPS)
             for t0, t1 in QUANT[step]
         }
-        x_words = held.tile([P, (STEPS + 1) * T], I32, name="x_words", align_bytes=64)
-        x_scales = held.tile([P, 2 * T], U8, name="x_scales", tag="x_scales", align_bytes=64)
+        x_words = held.tile([P, (STEPS - 1) * T + 4096], I32, name="x_words", align_bytes=64)
+        x_scales = held.tile([P, 2048], U8, name="x_scales", tag="x_scales", align_bytes=64)
         slot_scales = held.tile([P, SLOTS], U8, name="slot_scales", align_bytes=64)
         moved_scales = held.tile([P, SLOTS], U8, name="moved_scales", align_bytes=64)
         w8_t = held.tile([P, 2 * E, 4 * N], U8, name="w8_t", align_bytes=64)
@@ -80,7 +80,7 @@ def tile_moe_tk_lin_relu2_kernel(
         ident = held.tile([P, P], F32, name="ident")
         relu_t = held.tile([P, SLOTS], F32, name="relu_t")
         y_t = held.tile([P, SLOTS], F32, name="y_t")
-        gated_t = [[held.tile([P, STRETCH], F32, name=f"gated{h}_{r}") for r in range(TOP)] for h in range(STRETCHES)]
+        gated_t = [held.tile([P, TURNED], F32, name=f"gated{r}") for r in range(TOP)]
         summed = [held.tile([P, STRETCH // P, P], F32, name=f"summed{h}") for h in range(STRETCHES)]
         rest_gated = [held.tile([P, REST], F32, name=f"rest_gated{r}") for r in range(TOP)]
         rest_pair = held.tile([P, REST], F32, name="rest_pair")
@@ -90,8 +90,7 @@ def tile_moe_tk_lin_relu2_kernel(
 
         nc.gpsimd.memset(moved_scales[:].bitcast(I32), 0)
         make_identity(nc, ident[:])
-        nc.vector.memset(x_scales[:].bitcast(I32), 0)
-        nc.vector.memset(x_words[:, STEPS * T :], 0)
+        nc.vector.memset(x_scales[:, 0:T].bitcast(I32), 0)
         nc.vector.memset(w_scales[:].rearrange("p g n -> p (g n)").bitcast(I32), 0)
 
         x_rows = xT.rearrange("(a p j) t -> a p j t", a=STEPS, j=4)
@@ -144,27 +143,28 @@ def tile_moe_tk_lin_relu2_kernel(
             return slot_words[step, lo][:, s0 - lo : s1 - lo]
 
         def gather_words(step, s0, s1):
-            width = T if s1 - s0 <= SHORT else 2 * T
+            width = min(w for w in (T, 2 * T, 2048, 4096) if s1 - s0 <= (3 * w // 4 if w <= 2048 else w // 2))
             window = x_words[:, first_word(step) : first_word(step) + width].bitcast(U32)
             nc.vector.tensor_copy(words(step, s0, s1), window.indirect(offs_t[:, s0 // 16 : s1 // 16]))
 
-        for t0, t1 in ROUNDS[0]:
-            cut = t0 + (t1 - t0) * HEAD_EIGHTHS // 8
-            nc.scalar.activation(*round_views(0, cut, t1), ACT.Copy)
-            nc.vector.tensor_copy(*round_views(0, t0, cut))
+        for (t0, t1), share in zip(ROUNDS[0], HEAD_EIGHTHS):
+            cut = t0 + (t1 - t0) * share // 8
+            if cut < t1:
+                nc.scalar.activation(*round_views(0, cut, t1), ACT.Copy)
+            if cut > t0:
+                nc.vector.tensor_copy(*round_views(0, t0, cut))
             quantise(0, t0, t1)
         for step in range(1, STEPS):
             for t0, t1 in ROUNDS[step]:
                 nc.scalar.activation(*round_views(step, t0, t1), ACT.Copy)
 
-        for step, stop in ((0, SLOTS), (1, SLOTS), (2, EARLY)):
-            new_words(step, 0, stop - P)
-            for s0 in range(0, stop - P, HALF):
-                gather_words(step, s0, min(s0 + HALF, stop - P))
+        for step, cut, stop in ((0, LAST, SLOTS), (1, LAST, SLOTS), (2, HALF, EARLY)):
+            new_words(step, 0, cut)
+            gather_words(step, 0, cut)
             for t0, t1 in QUANT[step + 1]:
                 quantise(step + 1, t0, t1)
-            new_words(step, stop - P, stop, tag=f"x_f{step + 1}_{LOADS[step + 1][-1][0]}")
-            gather_words(step, stop - P, stop)
+            new_words(step, cut, stop, tag=f"x_f{step + 1}_{LOADS[step + 1][-1][0]}")
+            gather_words(step, cut, stop)
 
         def gather_scales(s0, s1):
             nc.vector.tensor_copy(slot_scales[:, s0:s1], x_scales[:].indirect(offs_t[:, s0 // 16 : s1 // 16]))
@@ -179,8 +179,8 @@ def tile_moe_tk_lin_relu2_kernel(
 
         def sums(s0, s1):
             if s0 < LAST:
-                return bank[s0 // C % 4][:, s0 // (4 * C) * C + s0 % C :][:, 0 : s1 - s0]
-            return bank[(s0 - LAST) // P][:, 0:P]
+                return bank[s0 % EARLY // C][:, s0 // EARLY * C + s0 % C :][:, 0 : s1 - s0]
+            return bank[3 + (s0 - LAST) // P][:, C : C + P]
 
         def multiply(step, s0, s1):
             matrix = 2 * (s0 // C) + ORDER[step] % 2
@@ -199,14 +199,10 @@ def tile_moe_tk_lin_relu2_kernel(
             for g0 in range(s0, s1, P):
                 multiply(step, g0, g0 + P)
 
-        def step_2(s0, s1):
-            gather_words(2, s0, s1)
-            multiply_narrow(2, s0, s1)
-
         def step_3(s0, s1):
             gather_words(3, s0, s1)
-            width = min(C, s1 - s0)
-            for g0 in range(s0, s1, width):
+            for g0 in range(s0, s1, C):
+                width = min(C, s1 - g0)
                 cols, bias = slice(g0, g0 + width), b_t[:, g0 // C : g0 // C + 1]
                 multiply(3, g0, g0 + width)
                 if g0 >= LAST:
@@ -222,24 +218,23 @@ def tile_moe_tk_lin_relu2_kernel(
                 multiply(0, e * C, (e + 1) * C)
                 multiply_narrow(1, e * C, (e + 1) * C)
 
-        gather_scales(0, HALF)
-        open_sums(0, 4)
-        multiply_narrow(2, 0, 4 * C)
-        gather_scales(HALF, SLOTS)
-        step_3(0, 2 * C)
+        gather_scales(0, EARLY)
+        open_sums(0, EARLY // C)
+        multiply_narrow(2, 0, EARLY)
+        gather_scales(EARLY, SLOTS)
         gate_t = held.tile([P, TOP, T], F32, name="gate_t", tag="x_scales", align_bytes=64)
         nc.sync.dma_start(out=gate_t[:], in_=gate.rearrange("r p t -> p r t"))
-        open_sums(4, 6)
-        multiply_narrow(2, 4 * C, EARLY)
-        step_3(2 * C, 5 * C)
-        open_sums(6, 8)
-        step_2(EARLY, LAST)
-        step_3(5 * C, 6 * C)
+        step_3(0, 2 * C)
+        step_3(2 * C, EARLY)
+        open_sums(EARLY // C, BANKS)
         multiply_narrow(0, LAST, SLOTS)
         multiply_narrow(1, LAST, SLOTS)
-        step_3(6 * C, 7 * C)
+        gather_words(2, EARLY, LAST)
+        multiply_narrow(2, EARLY, LAST)
+        step_3(5 * C, 7 * C)
         step_3(7 * C, LAST)
-        step_2(LAST, SLOTS)
+        gather_words(2, LAST, SLOTS)
+        multiply_narrow(2, LAST, SLOTS)
         step_3(LAST, LAST + P)
         step_3(LAST + P, SLOTS)
 
@@ -248,18 +243,23 @@ def tile_moe_tk_lin_relu2_kernel(
             nc.vector.tensor_tensor(dst, picked, gate_t[:, r, t0:t1], ALU.mult)
 
         blocks = STRETCH // P
+
+        def gather_and_add(r, t0, t1):
+            gather_gated(gated_t[r][:, t0:t1], r, t0, t1)
+            for c in range(t0 // P, t1 // P):
+                nc.tensor.matmul(
+                    bank[c][:, 0:P],
+                    gated_t[r][:, c * P : (c + 1) * P],
+                    ident[:],
+                    start=(r == 0),
+                    stop=(r == TOP - 1),
+                    is_transpose=True,
+                )
+
+        for r in range(TOP - 1):
+            gather_and_add(r, 0, TURNED)
         for h in range(STRETCHES):
-            for r in range(TOP):
-                gather_gated(gated_t[h][r][:], r, STRETCH * h, STRETCH * (h + 1))
-                for c in range(blocks):
-                    nc.tensor.matmul(
-                        bank[blocks * h + c][:, 0:P],
-                        gated_t[h][r][:, c * P : (c + 1) * P],
-                        ident[:],
-                        start=(r == 0),
-                        stop=(r == TOP - 1),
-                        is_transpose=True,
-                    )
+            gather_and_add(TOP - 1, STRETCH * h, STRETCH * (h + 1))
             back = bank[blocks * STRETCHES + h]
             for c in range(blocks):
                 nc.scalar.copy(summed[h][:, c, :], bank[blocks * h + c][:, 0:P])

@@ -21,7 +21,6 @@ ALU = mybir.AluOpType
 P = 128
 TOP = 3
 STEPS = 4
-BANKS = 8
 QUADRANTS = 4
 
 ORDER = (0, 2, 3, 1)
@@ -35,18 +34,21 @@ WIDE = ((0, 512), (512, 768))
 LOADS = (HEAD, THIRDS, WIDE, ((0, T),))
 ROUNDS = (HEAD, THIRDS, WIDE, WIDE)
 QUANT = (HEAD, WIDE, WIDE, WIDE)
-HEAD_EIGHTHS = (5, 5, 5, 5)
 
-HALF = SLOTS // 2
-SHORT = 3 * T // 4
-EARLY = HALF + P
-LAST = BANKS * C
-SQUARE = 512
+WINDOWS = ((3 * T // 4, T), (3 * T // 2, 2 * T), (2048, 4096))
+LONG, WIDEST = WINDOWS[-1]
+EARLY_EXPERTS = 5
+EARLY = EARLY_EXPERTS * C
+SCALE_WINDOW = 2048
+LAST = (E - 1) * C
+SQUARE = 2 * C
 
 STRETCH = 256
 STRETCHES = 2
 TURNED = STRETCHES * STRETCH
 REST = T - TURNED
+BLOCKS = STRETCH // P
+BANKS = TURNED // P + STRETCHES
 
 
 def tile_moe_tk_lin_relu2_kernel(
@@ -69,8 +71,8 @@ def tile_moe_tk_lin_relu2_kernel(
             for step in range(STEPS)
             for t0, t1 in QUANT[step]
         }
-        x_words = held.tile([P, (STEPS - 1) * T + 4096], I32, name="x_words", align_bytes=64)
-        x_scales = held.tile([P, 2048], U8, name="x_scales", tag="x_scales", align_bytes=64)
+        x_words = held.tile([P, (STEPS - 1) * T + WIDEST], I32, name="x_words", align_bytes=64)
+        x_scales = held.tile([P, SCALE_WINDOW], U8, name="x_scales", tag="x_scales", align_bytes=64)
         slot_scales = held.tile([P, SLOTS], U8, name="slot_scales", align_bytes=64)
         moved_scales = held.tile([P, SLOTS], U8, name="moved_scales", align_bytes=64)
         w8_t = held.tile([P, 2 * E, 4 * N], U8, name="w8_t", align_bytes=64)
@@ -81,7 +83,7 @@ def tile_moe_tk_lin_relu2_kernel(
         relu_t = held.tile([P, SLOTS], F32, name="relu_t")
         y_t = held.tile([P, SLOTS], F32, name="y_t")
         gated_t = [held.tile([P, TURNED], F32, name=f"gated{r}") for r in range(TOP)]
-        summed = [held.tile([P, STRETCH // P, P], F32, name=f"summed{h}") for h in range(STRETCHES)]
+        summed = [held.tile([P, BLOCKS, P], F32, name=f"summed{h}") for h in range(STRETCHES)]
         rest_gated = [held.tile([P, REST], F32, name=f"rest_gated{r}") for r in range(TOP)]
         rest_pair = held.tile([P, REST], F32, name="rest_pair")
         out_turned = [held.tile([P, STRETCH], F32, name=f"out_turned{h}") for h in range(STRETCHES)]
@@ -143,22 +145,20 @@ def tile_moe_tk_lin_relu2_kernel(
             return slot_words[step, lo][:, s0 - lo : s1 - lo]
 
         def gather_words(step, s0, s1):
-            width = min(w for w in (T, 2 * T, 2048, 4096) if s1 - s0 <= (3 * w // 4 if w <= 2048 else w // 2))
+            width = min(columns for longest, columns in WINDOWS if s1 - s0 <= longest)
             window = x_words[:, first_word(step) : first_word(step) + width].bitcast(U32)
             nc.vector.tensor_copy(words(step, s0, s1), window.indirect(offs_t[:, s0 // 16 : s1 // 16]))
 
-        for (t0, t1), share in zip(ROUNDS[0], HEAD_EIGHTHS):
-            cut = t0 + (t1 - t0) * share // 8
-            if cut < t1:
-                nc.scalar.activation(*round_views(0, cut, t1), ACT.Copy)
-            if cut > t0:
-                nc.vector.tensor_copy(*round_views(0, t0, cut))
+        for t0, t1 in ROUNDS[0]:
+            cut = (t0 + t1) // 2
+            nc.scalar.activation(*round_views(0, cut, t1), ACT.Copy)
+            nc.vector.tensor_copy(*round_views(0, t0, cut))
             quantise(0, t0, t1)
         for step in range(1, STEPS):
             for t0, t1 in ROUNDS[step]:
                 nc.scalar.activation(*round_views(step, t0, t1), ACT.Copy)
 
-        for step, cut, stop in ((0, LAST, SLOTS), (1, LAST, SLOTS), (2, HALF, EARLY)):
+        for step, cut, stop in ((0, LONG, SLOTS), (1, LONG, SLOTS), (2, EARLY - P, EARLY)):
             new_words(step, 0, cut)
             gather_words(step, 0, cut)
             for t0, t1 in QUANT[step + 1]:
@@ -174,13 +174,16 @@ def tile_moe_tk_lin_relu2_kernel(
                     out=moved_scales[32 * q : 32 * q + 4, s0:s1].bitcast(I32),
                     in_=slot_scales[row : row + 4, s0:s1].bitcast(I32),
                 )
+
         new_words(2, EARLY, SLOTS, tag=f"x_b3_{QUANT[3][-1][0]}")
         new_words(3, 0, SLOTS)
 
         def sums(s0, s1):
+            if s0 < EARLY:
+                return bank[s0 // C][:, s0 % C : s0 % C + s1 - s0]
             if s0 < LAST:
-                return bank[s0 % EARLY // C][:, s0 // EARLY * C + s0 % C :][:, 0 : s1 - s0]
-            return bank[3 + (s0 - LAST) // P][:, C : C + P]
+                return bank[(s0 - EARLY) // C][:, C + s0 % C : C + s0 % C + s1 - s0]
+            return bank[(LAST - EARLY) // C + (s0 - LAST) // P][:, C : C + P]
 
         def multiply(step, s0, s1):
             matrix = 2 * (s0 // C) + ORDER[step] % 2
@@ -198,6 +201,10 @@ def tile_moe_tk_lin_relu2_kernel(
         def multiply_narrow(step, s0, s1):
             for g0 in range(s0, s1, P):
                 multiply(step, g0, g0 + P)
+
+        def step_2(s0, s1):
+            gather_words(2, s0, s1)
+            multiply_narrow(2, s0, s1)
 
         def step_3(s0, s1):
             gather_words(3, s0, s1)
@@ -219,30 +226,26 @@ def tile_moe_tk_lin_relu2_kernel(
                 multiply_narrow(1, e * C, (e + 1) * C)
 
         gather_scales(0, EARLY)
-        open_sums(0, EARLY // C)
+        open_sums(0, EARLY_EXPERTS)
         multiply_narrow(2, 0, EARLY)
         gather_scales(EARLY, SLOTS)
         gate_t = held.tile([P, TOP, T], F32, name="gate_t", tag="x_scales", align_bytes=64)
         nc.sync.dma_start(out=gate_t[:], in_=gate.rearrange("r p t -> p r t"))
         step_3(0, 2 * C)
         step_3(2 * C, EARLY)
-        open_sums(EARLY // C, BANKS)
+        open_sums(EARLY_EXPERTS, E - 1)
         multiply_narrow(0, LAST, SLOTS)
         multiply_narrow(1, LAST, SLOTS)
-        gather_words(2, EARLY, LAST)
-        multiply_narrow(2, EARLY, LAST)
-        step_3(5 * C, 7 * C)
-        step_3(7 * C, LAST)
-        gather_words(2, LAST, SLOTS)
-        multiply_narrow(2, LAST, SLOTS)
+        step_2(EARLY, LAST)
+        step_3(EARLY, LAST - C)
+        step_3(LAST - C, LAST)
+        step_2(LAST, SLOTS)
         step_3(LAST, LAST + P)
         step_3(LAST + P, SLOTS)
 
         def gather_gated(dst, r, t0, t1):
             picked = y_t[:].indirect(pos_t[r][:, t0 // 16 : t1 // 16])
             nc.vector.tensor_tensor(dst, picked, gate_t[:, r, t0:t1], ALU.mult)
-
-        blocks = STRETCH // P
 
         def gather_and_add(r, t0, t1):
             gather_gated(gated_t[r][:, t0:t1], r, t0, t1)
@@ -260,9 +263,9 @@ def tile_moe_tk_lin_relu2_kernel(
             gather_and_add(r, 0, TURNED)
         for h in range(STRETCHES):
             gather_and_add(TOP - 1, STRETCH * h, STRETCH * (h + 1))
-            back = bank[blocks * STRETCHES + h]
-            for c in range(blocks):
-                nc.scalar.copy(summed[h][:, c, :], bank[blocks * h + c][:, 0:P])
+            back = bank[BLOCKS * STRETCHES + h]
+            for c in range(BLOCKS):
+                nc.scalar.copy(summed[h][:, c, :], bank[BLOCKS * h + c][:, 0:P])
                 nc.tensor.transpose(back[:, c * P : (c + 1) * P], summed[h][:, c, :], ident[:])
             nc.scalar.copy(out_turned[h][:], back[:, 0:STRETCH])
             nc.scalar.dma_start(out=out[:, STRETCH * h : STRETCH * (h + 1)], in_=out_turned[h][:])

@@ -227,12 +227,12 @@ def tile_moe_tk_lin_relu2_kernel(
 
         gather_scales(0, EARLY)
         open_sums(0, EARLY_EXPERTS)
-        multiply_narrow(2, 0, EARLY)
         gather_scales(EARLY, SLOTS)
         gate_t = held.tile([P, TOP, T], F32, name="gate_t", tag="x_scales", align_bytes=64)
         nc.sync.dma_start(out=gate_t[:], in_=gate.rearrange("r p t -> p r t"))
-        step_3(0, 2 * C)
-        step_3(2 * C, EARLY)
+        for s0, s1 in ((0, 2 * C), (2 * C, EARLY)):
+            multiply_narrow(2, s0, s1)
+            step_3(s0, s1)
         open_sums(EARLY_EXPERTS, E - 1)
         multiply_narrow(0, LAST, SLOTS)
         multiply_narrow(1, LAST, SLOTS)

@@ -208,17 +208,21 @@ def tile_moe_tk_lin_relu2_kernel(
 
         def step_3(s0, s1):
             gather_words(3, s0, s1)
-            for g0 in range(s0, s1, C):
-                width = min(C, s1 - g0)
-                cols, bias = slice(g0, g0 + width), b_t[:, g0 // C : g0 // C + 1]
-                multiply(3, g0, g0 + width)
-                if g0 >= LAST:
-                    nc.vector.tensor_scalar(relu_t[:, cols], sums(g0, g0 + width), bias, 0.0, ALU.add, ALU.max)
-                else:
-                    nc.scalar.activation(relu_t[:, cols], sums(g0, g0 + width), ACT.Relu, bias=bias)
+            for e in range(s0 // C, s1 // C):
+                cols = slice(e * C, (e + 1) * C)
+                multiply(3, e * C, (e + 1) * C)
+                nc.scalar.activation(relu_t[:, cols], sums(e * C, (e + 1) * C), ACT.Relu, bias=b_t[:, e : e + 1])
             for q0 in range(s0, s1, SQUARE):
                 q1 = min(q0 + SQUARE, s1)
                 nc.scalar.activation(y_t[:, q0:q1], relu_t[:, q0:q1], ACT.Square)
+
+        def step_3_last(s0, width):
+            gather_words(3, s0, s0 + P)
+            multiply(3, s0, s0 + P)
+            for q0 in range(0, P, width):
+                cols, half_sums = slice(s0 + q0, s0 + q0 + width), sums(s0, s0 + P)[:, q0 : q0 + width]
+                nc.vector.tensor_scalar(relu_t[:, cols], half_sums, b_t[:, E - 1 : E], 0.0, ALU.add, ALU.max)
+                nc.scalar.activation(y_t[:, cols], relu_t[:, cols], ACT.Square)
 
         def open_sums(e0, e1):
             for e in range(e0, e1):
@@ -240,8 +244,8 @@ def tile_moe_tk_lin_relu2_kernel(
         step_3(EARLY, LAST - C)
         step_3(LAST - C, LAST)
         step_2(LAST, SLOTS)
-        step_3(LAST, LAST + P)
-        step_3(LAST + P, SLOTS)
+        step_3_last(LAST, P)
+        step_3_last(LAST + P, P // 2)
 
         def gather_gated(dst, r, t0, t1):
             picked = y_t[:].indirect(pos_t[r][:, t0 // 16 : t1 // 16])

@@ -93,7 +93,8 @@ def tile_moe_tk_lin_relu2_kernel(
         nc.gpsimd.memset(moved_scales[:].bitcast(I32), 0)
         make_identity(nc, ident[:])
         nc.vector.memset(x_scales[:, 0:T].bitcast(I32), 0)
-        nc.vector.memset(w_scales[:].rearrange("p g n -> p (g n)").bitcast(I32), 0)
+        for g0 in (0, E):
+            nc.vector.memset(w_scales[:, g0 : g0 + E, :].rearrange("p g n -> p (g n)").bitcast(I32), 0)
 
         x_rows = xT.rearrange("(a p j) t -> a p j t", a=STEPS, j=4)
 

@@ -112,8 +112,11 @@ def tile_moe_tk_lin_relu2_kernel(
                     out=w_scales[32 * q + first : 32 * q + first + 4].bitcast(I32),
                     in_=scales[:, :, 4 * q : 4 * q + 4, :].rearrange("e a q n -> q (e a) n").bitcast(I32),
                 )
-        nc.sync.dma_start(out=w8_t[:].bitcast(I32), in_=w8_words.rearrange("e a p n r -> p (e a) (n r)").bitcast(I32))
-        nc.sync.dma_start(out=w4_t[:].bitcast(I32), in_=w4_words.rearrange("e a p n -> p (e a) n").bitcast(I32))
+        w8_rows = w8_words.rearrange("e a p n r -> p (e a) (n r)").bitcast(I32)
+        w4_rows = w4_words.rearrange("e a p n -> p (e a) n").bitcast(I32)
+        for g0, g1 in ((0, 2 * EARLY_EXPERTS), (2 * EARLY_EXPERTS, 2 * E)):
+            nc.sync.dma_start(out=w8_t[:, g0:g1, :].bitcast(I32), in_=w8_rows[:, g0:g1, :])
+            nc.sync.dma_start(out=w4_t[:, g0:g1, :].bitcast(I32), in_=w4_rows[:, g0:g1, :])
         nc.sync.dma_start(out=b_t[:], in_=b)
         for pos_tile, pos in zip(pos_t, (pos1, pos2, pos3)):
             nc.sync.dma_start(pos_tile[:], pos)

@@ -90,11 +90,10 @@ def tile_moe_tk_lin_relu2_kernel(
         out_rest = held.tile([P, REST], F32, name="out_rest")
         bank = [psum.tile([P, 512], F32, name=f"bank{i}") for i in range(BANKS)]
 
-        nc.gpsimd.memset(moved_scales[:].bitcast(I32), 0)
         make_identity(nc, ident[:])
         nc.vector.memset(x_scales[:, 0:T].bitcast(I32), 0)
-        for g0 in (0, E):
-            nc.vector.memset(w_scales[:, g0 : g0 + E, :].rearrange("p g n -> p (g n)").bitcast(I32), 0)
+        nc.vector.memset(w_scales[:].rearrange("p g n -> p (g n)").bitcast(I32), 0)
+        nc.vector.memset(moved_scales[:].bitcast(I32), 0)
 
         x_rows = xT.rearrange("(a p j) t -> a p j t", a=STEPS, j=4)
 

@@ -1,7 +1,6 @@
 from contextlib import ExitStack
 
 import concourse.mybir as mybir
-from concourse.masks import make_identity
 
 K, T, E, C, N = 2048, 768, 9, 256, 128
 SLOTS = E * C
@@ -43,12 +42,9 @@ SCALE_WINDOW = 2048
 LAST = (E - 1) * C
 SQUARE = 2 * C
 
-STRETCH = 256
-STRETCHES = 2
-TURNED = STRETCHES * STRETCH
-REST = T - TURNED
-BLOCKS = STRETCH // P
-BANKS = TURNED // P + STRETCHES
+FUSED = 640
+PIECES = ((0, 256), (256, 512), (512, 640), (640, 768))
+BANKS = EARLY_EXPERTS
 
 
 def tile_moe_tk_lin_relu2_kernel(
@@ -79,18 +75,15 @@ def tile_moe_tk_lin_relu2_kernel(
         w4_t = held.tile([P, 2 * E, 2 * N], U8, name="w4_t", align_bytes=64)
         w_scales = held.tile([P, 2 * E, N], U8, name="w_scales", align_bytes=64)
         b_t = held.tile([P, E], F32, name="b_t")
-        ident = held.tile([P, P], F32, name="ident")
         relu_t = held.tile([P, SLOTS], F32, name="relu_t")
         y_t = held.tile([P, SLOTS], F32, name="y_t")
-        gated_t = [held.tile([P, TURNED], F32, name=f"gated{r}") for r in range(TOP)]
-        summed = [held.tile([P, BLOCKS, P], F32, name=f"summed{h}") for h in range(STRETCHES)]
-        rest_gated = [held.tile([P, REST], F32, name=f"rest_gated{r}") for r in range(TOP)]
-        rest_pair = held.tile([P, REST], F32, name="rest_pair")
-        out_turned = [held.tile([P, STRETCH], F32, name=f"out_turned{h}") for h in range(STRETCHES)]
-        out_rest = held.tile([P, REST], F32, name="out_rest")
+        fused = held.tile([P, FUSED], F32, name="fused")
+        picked = {t0: held.tile([P, TOP, t1 - t0], F32, name=f"picked{t0}") for t0, t1 in PIECES}
+        gated = {t0: held.tile([P, TOP, t1 - t0], F32, name=f"gated{t0}") for t0, t1 in PIECES}
+        pair = {t0: held.tile([P, t1 - t0], F32, name=f"pair{t0}") for t0, t1 in PIECES}
+        out_t = {t0: held.tile([P, t1 - t0], F32, name=f"out_t{t0}") for t0, t1 in PIECES}
         bank = [psum.tile([P, 512], F32, name=f"bank{i}") for i in range(BANKS)]
 
-        make_identity(nc, ident[:])
         nc.vector.memset(x_scales[:, 0:T].bitcast(I32), 0)
         nc.vector.memset(w_scales[:].rearrange("p g n -> p (g n)").bitcast(I32), 0)
         nc.vector.memset(moved_scales[:].bitcast(I32), 0)
@@ -250,39 +243,40 @@ def tile_moe_tk_lin_relu2_kernel(
         step_3_last(LAST, P)
         step_3_last(LAST + P, P // 2)
 
-        def gather_gated(dst, r, t0, t1):
-            picked = y_t[:].indirect(pos_t[r][:, t0 // 16 : t1 // 16])
-            nc.vector.tensor_tensor(dst, picked, gate_t[:, r, t0:t1], ALU.mult)
+        def results(r, t0, t1):
+            return y_t[:].indirect(pos_t[r][:, t0 // 16 : t1 // 16])
 
-        def gather_and_add(r, t0, t1):
-            gather_gated(gated_t[r][:, t0:t1], r, t0, t1)
-            for c in range(t0 // P, t1 // P):
-                nc.tensor.matmul(
-                    bank[c][:, 0:P],
-                    gated_t[r][:, c * P : (c + 1) * P],
-                    ident[:],
-                    start=(r == 0),
-                    stop=(r == TOP - 1),
-                    is_transpose=True,
-                )
+        for t0, t1 in PIECES:
+            for r in range(1 if t0 < FUSED else 0, TOP):
+                nc.scalar.activation(picked[t0][:, r, :], results(r, t0, t1), ACT.Copy)
+        nc.vector.tensor_tensor(fused[:], results(0, 0, FUSED), gate_t[:, 0, 0:FUSED], ALU.mult)
 
-        for r in range(TOP - 1):
-            gather_and_add(r, 0, TURNED)
-        for h in range(STRETCHES):
-            gather_and_add(TOP - 1, STRETCH * h, STRETCH * (h + 1))
-            back = bank[BLOCKS * STRETCHES + h]
-            for c in range(BLOCKS):
-                nc.scalar.copy(summed[h][:, c, :], bank[BLOCKS * h + c][:, 0:P])
-                nc.tensor.transpose(back[:, c * P : (c + 1) * P], summed[h][:, c, :], ident[:])
-            nc.scalar.copy(out_turned[h][:], back[:, 0:STRETCH])
-            nc.scalar.dma_start(out=out[:, STRETCH * h : STRETCH * (h + 1)], in_=out_turned[h][:])
+        def product(piece, r0, r1):
+            t0, t1 = PIECES[piece]
+            nc.vector.tensor_tensor(gated[t0][:, r0:r1, :], picked[t0][:, r0:r1, :], gate_t[:, r0:r1, t0:t1], ALU.mult)
 
-        mid = REST // 2
-        gather_gated(rest_gated[0][:], 0, TURNED, T)
-        gather_gated(rest_gated[1][:], 1, TURNED, T)
-        gather_gated(rest_gated[2][:, 0:mid], 2, TURNED, TURNED + mid)
-        nc.vector.tensor_tensor(rest_pair[:], rest_gated[0][:], rest_gated[1][:], ALU.add)
-        gather_gated(rest_gated[2][:, mid:], 2, TURNED + mid, T)
-        for c0, c1 in ((0, mid), (mid, REST)):
-            nc.vector.tensor_tensor(out_rest[:, c0:c1], rest_pair[:, c0:c1], rest_gated[2][:, c0:c1], ALU.add)
-            nc.sync.dma_start(out=out[:, TURNED + c0 : TURNED + c1], in_=out_rest[:, c0:c1])
+        def add_pair(piece):
+            t0, t1 = PIECES[piece]
+            first = fused[:, t0:t1] if t0 < FUSED else gated[t0][:, 0, :]
+            nc.vector.tensor_tensor(pair[t0][:], first, gated[t0][:, 1, :], ALU.add)
+
+        def finish(piece):
+            t0, t1 = PIECES[piece]
+            nc.vector.tensor_tensor(out_t[t0][:], pair[t0][:], gated[t0][:, 2, :], ALU.add)
+            nc.sync.dma_start(out=out[:, t0:t1], in_=out_t[t0][:])
+
+        product(0, 1, 2)
+        product(0, 2, 3)
+        add_pair(0)
+        product(1, 1, 2)
+        finish(0)
+        product(1, 2, 3)
+        add_pair(1)
+        product(2, 1, 3)
+        finish(1)
+        add_pair(2)
+        product(3, 0, 2)
+        finish(2)
+        product(3, 2, 3)
+        add_pair(3)
+        finish(3)

@@ -1,6 +1,7 @@
 from contextlib import ExitStack
 
 import concourse.mybir as mybir
+from concourse.masks import make_identity
 
 K, T, E, C, N = 2048, 768, 9, 256, 128
 SLOTS = E * C
@@ -30,7 +31,7 @@ W8_PLANE = 8
 HEAD = ((0, 256), (256, 512), (512, 640), (640, 768))
 THIRDS = ((0, 256), (256, 512), (512, 768))
 WIDE = ((0, 512), (512, 768))
-LOADS = (HEAD, THIRDS, WIDE, ((0, T),))
+LOADS = (HEAD, THIRDS, ((0, T),), ((0, T),))
 ROUNDS = (HEAD, THIRDS, WIDE, WIDE)
 QUANT = (HEAD, WIDE, WIDE, WIDE)
 
@@ -42,9 +43,12 @@ SCALE_WINDOW = 2048
 LAST = (E - 1) * C
 SQUARE = 2 * C
 
-FUSED = 640
-PIECES = ((0, 256), (256, 512), (512, 640), (640, 768))
-BANKS = EARLY_EXPERTS
+BLOCKS = 3
+TURNED = BLOCKS * P
+REST = T - TURNED
+TURNED_PIECES = ((0, 256), (256, 384))
+REST_PIECES = ((0, 256), (256, 384))
+BANKS = 8
 
 
 def tile_moe_tk_lin_relu2_kernel(
@@ -77,13 +81,17 @@ def tile_moe_tk_lin_relu2_kernel(
         b_t = held.tile([P, E], F32, name="b_t")
         relu_t = held.tile([P, SLOTS], F32, name="relu_t")
         y_t = held.tile([P, SLOTS], F32, name="y_t")
-        fused = held.tile([P, FUSED], F32, name="fused")
-        picked = {t0: held.tile([P, TOP, t1 - t0], F32, name=f"picked{t0}") for t0, t1 in PIECES}
-        gated = {t0: held.tile([P, TOP, t1 - t0], F32, name=f"gated{t0}") for t0, t1 in PIECES}
-        pair = {t0: held.tile([P, t1 - t0], F32, name=f"pair{t0}") for t0, t1 in PIECES}
-        out_t = {t0: held.tile([P, t1 - t0], F32, name=f"out_t{t0}") for t0, t1 in PIECES}
+        ident = held.tile([P, P], F32, name="ident")
+        gate_cols = [held.tile([P, BLOCKS], F32, name=f"gate_cols{r}") for r in range(TOP - 1)]
+        fused = held.tile([P, TURNED], F32, name="fused")
+        picked = [held.tile([P, TURNED], F32, name=f"picked{r}") for r in range(TOP - 1)]
+        scaled = [held.tile([P, BLOCKS, P], F32, name=f"scaled{r}") for r in range(TOP - 1)]
+        rest_gated = [held.tile([P, REST], F32, name=f"rest_gated{r}") for r in range(TOP)]
+        rest_pair = held.tile([P, REST], F32, name="rest_pair")
+        out_t = held.tile([P, T], F32, name="out_t")
         bank = [psum.tile([P, 512], F32, name=f"bank{i}") for i in range(BANKS)]
 
+        make_identity(nc, ident[:])
         nc.vector.memset(x_scales[:, 0:T].bitcast(I32), 0)
         nc.vector.memset(w_scales[:].rearrange("p g n -> p (g n)").bitcast(I32), 0)
         nc.vector.memset(moved_scales[:].bitcast(I32), 0)
@@ -104,14 +112,14 @@ def tile_moe_tk_lin_relu2_kernel(
                     out=w_scales[32 * q + first : 32 * q + first + 4].bitcast(I32),
                     in_=scales[:, :, 4 * q : 4 * q + 4, :].rearrange("e a q n -> q (e a) n").bitcast(I32),
                 )
-        w8_rows = w8_words.rearrange("e a p n r -> p (e a) (n r)").bitcast(I32)
-        w4_rows = w4_words.rearrange("e a p n -> p (e a) n").bitcast(I32)
-        for g0, g1 in ((0, 2 * EARLY_EXPERTS), (2 * EARLY_EXPERTS, 2 * E)):
-            nc.sync.dma_start(out=w8_t[:, g0:g1, :].bitcast(I32), in_=w8_rows[:, g0:g1, :])
-            nc.sync.dma_start(out=w4_t[:, g0:g1, :].bitcast(I32), in_=w4_rows[:, g0:g1, :])
+        nc.sync.dma_start(out=w8_t[:].bitcast(I32), in_=w8_words.rearrange("e a p n r -> p (e a) (n r)").bitcast(I32))
+        nc.sync.dma_start(out=w4_t[:].bitcast(I32), in_=w4_words.rearrange("e a p n -> p (e a) n").bitcast(I32))
         nc.sync.dma_start(out=b_t[:], in_=b)
         for pos_tile, pos in zip(pos_t, (pos1, pos2, pos3)):
             nc.sync.dma_start(pos_tile[:], pos)
+        with nc.allow_non_contiguous_dma(reason="one gate value a partition"):
+            for r in range(TOP - 1):
+                nc.sync.dma_start(out=gate_cols[r][:], in_=gate[r + 1, 0, 0:TURNED].rearrange("(c p) -> p c", p=P))
 
         def round_views(step, t0, t1):
             f0 = max(lo for lo, hi in LOADS[step] if lo <= t0)
@@ -228,8 +236,11 @@ def tile_moe_tk_lin_relu2_kernel(
         gather_scales(0, EARLY)
         open_sums(0, EARLY_EXPERTS)
         gather_scales(EARLY, SLOTS)
-        gate_t = held.tile([P, TOP, T], F32, name="gate_t", tag="x_scales", align_bytes=64)
-        nc.sync.dma_start(out=gate_t[:], in_=gate.rearrange("r p t -> p r t"))
+        gate_t = held.tile([P, T + 2 * REST], F32, name="gate_t", tag="x_scales", align_bytes=64)
+        nc.sync.dma_start(out=gate_t[:, 0:T], in_=gate[0])
+        nc.sync.dma_start(
+            out=gate_t[:, T:].rearrange("p (r t) -> p r t", r=2), in_=gate[1:TOP, :, TURNED:T].rearrange("r p t -> p r t")
+        )
         for s0, s1 in ((0, 2 * C), (2 * C, EARLY)):
             multiply_narrow(2, s0, s1)
             step_3(s0, s1)
@@ -246,37 +257,65 @@ def tile_moe_tk_lin_relu2_kernel(
         def results(r, t0, t1):
             return y_t[:].indirect(pos_t[r][:, t0 // 16 : t1 // 16])
 
-        for t0, t1 in PIECES:
-            for r in range(1 if t0 < FUSED else 0, TOP):
-                nc.scalar.activation(picked[t0][:, r, :], results(r, t0, t1), ACT.Copy)
-        nc.vector.tensor_tensor(fused[:], results(0, 0, FUSED), gate_t[:, 0, 0:FUSED], ALU.mult)
+        def rest_gate(r):
+            return gate_t[:, TURNED:T] if r == 0 else gate_t[:, T + (r - 1) * REST : T + r * REST]
 
-        def product(piece, r0, r1):
-            t0, t1 = PIECES[piece]
-            nc.vector.tensor_tensor(gated[t0][:, r0:r1, :], picked[t0][:, r0:r1, :], gate_t[:, r0:r1, t0:t1], ALU.mult)
+        for r in range(TOP - 1):
+            nc.scalar.activation(picked[r][:], results(r + 1, 0, TURNED), ACT.Copy)
+            for c in range(BLOCKS):
+                nc.tensor.transpose(bank[5 + r][:, c * P : (c + 1) * P], picked[r][:, c * P : (c + 1) * P], ident[:])
+        for r in range(TOP - 1):
+            for c in range(BLOCKS):
+                nc.scalar.activation(
+                    scaled[r][:, c, :], bank[5 + r][:, c * P : (c + 1) * P], ACT.Copy, scale=gate_cols[r][:, c : c + 1]
+                )
+        for h, (t0, t1) in enumerate(TURNED_PIECES):
+            for c in range(t0 // P, t1 // P):
+                for r in range(TOP - 1):
+                    nc.tensor.matmul(
+                        bank[h][:, c * P - t0 : (c + 1) * P - t0],
+                        scaled[r][:, c, :],
+                        ident[:],
+                        start=(r == 0),
+                        stop=(r == TOP - 2),
+                        is_transpose=True,
+                    )
+        rest_picked = [
+            held.tile([P, c1 - c0], F32, name=f"rest_picked{c0}", tag=tag)
+            for (c0, c1), tag in zip(REST_PIECES, ("rest_picked", "picked1"))
+        ]
+        for h, (c0, c1) in enumerate(REST_PIECES):
+            nc.scalar.activation(rest_picked[h][:], results(TOP - 1, TURNED + c0, TURNED + c1), ACT.Copy)
 
-        def add_pair(piece):
-            t0, t1 = PIECES[piece]
-            first = fused[:, t0:t1] if t0 < FUSED else gated[t0][:, 0, :]
-            nc.vector.tensor_tensor(pair[t0][:], first, gated[t0][:, 1, :], ALU.add)
+        for r in range(TOP - 1):
+            nc.vector.tensor_tensor(rest_gated[r][:], results(r, TURNED, T), rest_gate(r), ALU.mult)
+        nc.vector.tensor_tensor(fused[:], results(0, 0, TURNED), gate_t[:, 0:TURNED], ALU.mult)
 
-        def finish(piece):
-            t0, t1 = PIECES[piece]
-            nc.vector.tensor_tensor(out_t[t0][:], pair[t0][:], gated[t0][:, 2, :], ALU.add)
-            nc.sync.dma_start(out=out[:, t0:t1], in_=out_t[t0][:])
+        def finish(t0, t1, one, other):
+            nc.vector.tensor_tensor(out_t[:, t0:t1], one, other, ALU.add)
+            nc.sync.dma_start(out=out[:, t0:t1], in_=out_t[:, t0:t1])
 
-        product(0, 1, 2)
-        product(0, 2, 3)
+        def add_pair(h):
+            c0, c1 = REST_PIECES[h]
+            nc.vector.tensor_tensor(rest_pair[:, c0:c1], rest_gated[0][:, c0:c1], rest_gated[1][:, c0:c1], ALU.add)
+
+        def product(h):
+            c0, c1 = REST_PIECES[h]
+            nc.vector.tensor_tensor(rest_gated[2][:, c0:c1], rest_picked[h][:], rest_gate(2)[:, c0:c1], ALU.mult)
+
+        def finish_rest(h):
+            c0, c1 = REST_PIECES[h]
+            finish(TURNED + c0, TURNED + c1, rest_pair[:, c0:c1], rest_gated[2][:, c0:c1])
+
+        def finish_turned(h):
+            t0, t1 = TURNED_PIECES[h]
+            finish(t0, t1, bank[h][:, 0 : t1 - t0], fused[:, t0:t1])
+
         add_pair(0)
-        product(1, 1, 2)
-        finish(0)
-        product(1, 2, 3)
+        product(0)
         add_pair(1)
-        product(2, 1, 3)
-        finish(1)
-        add_pair(2)
-        product(3, 0, 2)
-        finish(2)
-        product(3, 2, 3)
-        add_pair(3)
-        finish(3)
+        finish_rest(0)
+        finish_turned(0)
+        product(1)
+        finish_turned(1)
+        finish_rest(1)

@@ -46,7 +46,6 @@ SQUARE = 2 * C
 BLOCKS = 3
 TURNED = BLOCKS * P
 REST = T - TURNED
-TURNED_PIECES = ((0, 256), (256, 384))
 REST_PIECES = ((0, 256), (256, 384))
 BANKS = 8
 
@@ -86,7 +85,7 @@ def tile_moe_tk_lin_relu2_kernel(
         fused = held.tile([P, TURNED], F32, name="fused")
         picked = [held.tile([P, TURNED], F32, name=f"picked{r}") for r in range(TOP - 1)]
         scaled = [held.tile([P, BLOCKS, P], F32, name=f"scaled{r}") for r in range(TOP - 1)]
-        rest_gated = [held.tile([P, REST], F32, name=f"rest_gated{r}") for r in range(TOP)]
+        rest_gated = [held.tile([P, w], F32, name=f"rest_gated{r}") for r, w in enumerate((REST, REST, REST))]
         rest_pair = held.tile([P, REST], F32, name="rest_pair")
         out_t = held.tile([P, T], F32, name="out_t")
         bank = [psum.tile([P, 512], F32, name=f"bank{i}") for i in range(BANKS)]
@@ -269,17 +268,11 @@ def tile_moe_tk_lin_relu2_kernel(
                 nc.scalar.activation(
                     scaled[r][:, c, :], bank[5 + r][:, c * P : (c + 1) * P], ACT.Copy, scale=gate_cols[r][:, c : c + 1]
                 )
-        for h, (t0, t1) in enumerate(TURNED_PIECES):
-            for c in range(t0 // P, t1 // P):
-                for r in range(TOP - 1):
-                    nc.tensor.matmul(
-                        bank[h][:, c * P - t0 : (c + 1) * P - t0],
-                        scaled[r][:, c, :],
-                        ident[:],
-                        start=(r == 0),
-                        stop=(r == TOP - 2),
-                        is_transpose=True,
-                    )
+        for r in range(TOP - 1):
+            for c in range(BLOCKS):
+                nc.tensor.matmul(
+                    bank[c][:, 0:P], scaled[r][:, c, :], ident[:], start=(r == 0), stop=(r == TOP - 2), is_transpose=True
+                )
         rest_picked = [
             held.tile([P, c1 - c0], F32, name=f"rest_picked{c0}", tag=tag)
             for (c0, c1), tag in zip(REST_PIECES, ("rest_picked", "picked1"))
@@ -291,31 +284,36 @@ def tile_moe_tk_lin_relu2_kernel(
             nc.vector.tensor_tensor(rest_gated[r][:], results(r, TURNED, T), rest_gate(r), ALU.mult)
         nc.vector.tensor_tensor(fused[:], results(0, 0, TURNED), gate_t[:, 0:TURNED], ALU.mult)
 
-        def finish(t0, t1, one, other):
-            nc.vector.tensor_tensor(out_t[:, t0:t1], one, other, ALU.add)
-            nc.sync.dma_start(out=out[:, t0:t1], in_=out_t[:, t0:t1])
-
         def add_pair(h):
             c0, c1 = REST_PIECES[h]
             nc.vector.tensor_tensor(rest_pair[:, c0:c1], rest_gated[0][:, c0:c1], rest_gated[1][:, c0:c1], ALU.add)
 
+        third = [rest_gated[2][:, c0:c1] for c0, c1 in REST_PIECES]
+
         def product(h):
             c0, c1 = REST_PIECES[h]
-            nc.vector.tensor_tensor(rest_gated[2][:, c0:c1], rest_picked[h][:], rest_gate(2)[:, c0:c1], ALU.mult)
+            nc.vector.tensor_tensor(third[h], rest_picked[h][:], rest_gate(2)[:, c0:c1], ALU.mult)
+
+        def store(t0, t1):
+            nc.sync.dma_start(out=out[:, t0:t1], in_=out_t[:, t0:t1])
 
         def finish_rest(h):
             c0, c1 = REST_PIECES[h]
-            finish(TURNED + c0, TURNED + c1, rest_pair[:, c0:c1], rest_gated[2][:, c0:c1])
+            nc.vector.tensor_tensor(out_t[:, TURNED + c0 : TURNED + c1], rest_pair[:, c0:c1], third[h], ALU.add)
+            store(TURNED + c0, TURNED + c1)
 
-        def finish_turned(h):
-            t0, t1 = TURNED_PIECES[h]
-            finish(t0, t1, bank[h][:, 0 : t1 - t0], fused[:, t0:t1])
+        def finish_block(c):
+            cols = slice(c * P, (c + 1) * P)
+            nc.vector.tensor_tensor(out_t[:, cols], bank[c][:, 0:P], fused[:, cols], ALU.add)
 
         add_pair(0)
         product(0)
         add_pair(1)
         finish_rest(0)
-        finish_turned(0)
+        finish_block(0)
         product(1)
-        finish_turned(1)
+        finish_block(1)
+        store(0, 2 * P)
         finish_rest(1)
+        finish_block(2)
+        store(2 * P, TURNED)

@@ -46,6 +46,7 @@ SQUARE = 2 * C
 BLOCKS = 3
 TURNED = BLOCKS * P
 REST = T - TURNED
+TURNED_PIECES = ((0, 2), (2, 3))
 REST_PIECES = ((0, 256), (256, 384))
 BANKS = 8
 
@@ -83,7 +84,11 @@ def tile_moe_tk_lin_relu2_kernel(
         ident = held.tile([P, P], F32, name="ident")
         gate_cols = [held.tile([P, BLOCKS], F32, name=f"gate_cols{r}") for r in range(TOP - 1)]
         fused = held.tile([P, TURNED], F32, name="fused")
-        picked = [held.tile([P, TURNED], F32, name=f"picked{r}") for r in range(TOP - 1)]
+        picked = {
+            (c0, r): held.tile([P, (c1 - c0) * P], F32, name=f"picked{c0}_{r}")
+            for c0, c1 in TURNED_PIECES
+            for r in range(TOP - 1)
+        }
         scaled = [held.tile([P, BLOCKS, P], F32, name=f"scaled{r}") for r in range(TOP - 1)]
         rest_gated = [held.tile([P, w], F32, name=f"rest_gated{r}") for r, w in enumerate((REST, REST, REST))]
         rest_pair = held.tile([P, REST], F32, name="rest_pair")
@@ -161,7 +166,7 @@ def tile_moe_tk_lin_relu2_kernel(
             for t0, t1 in ROUNDS[step]:
                 nc.scalar.activation(*round_views(step, t0, t1), ACT.Copy)
 
-        for step, cut, stop in ((0, LONG, SLOTS), (1, LONG, SLOTS), (2, EARLY - P, EARLY)):
+        for step, cut, stop in ((0, LONG, SLOTS), (1, LONG, SLOTS), (2, EARLY - C, EARLY)):
             new_words(step, 0, cut)
             gather_words(step, 0, cut)
             for t0, t1 in QUANT[step + 1]:
@@ -202,8 +207,9 @@ def tile_moe_tk_lin_relu2_kernel(
             )
 
         def multiply_narrow(step, s0, s1):
-            for g0 in range(s0, s1, P):
-                multiply(step, g0, g0 + P)
+            width = C if s0 < LAST else P
+            for g0 in range(s0, s1, width):
+                multiply(step, g0, g0 + width)
 
         def step_2(s0, s1):
             gather_words(2, s0, s1)
@@ -259,26 +265,30 @@ def tile_moe_tk_lin_relu2_kernel(
         def rest_gate(r):
             return gate_t[:, TURNED:T] if r == 0 else gate_t[:, T + (r - 1) * REST : T + r * REST]
 
-        for r in range(TOP - 1):
-            nc.scalar.activation(picked[r][:], results(r + 1, 0, TURNED), ACT.Copy)
-            for c in range(BLOCKS):
-                nc.tensor.transpose(bank[5 + r][:, c * P : (c + 1) * P], picked[r][:, c * P : (c + 1) * P], ident[:])
-        for r in range(TOP - 1):
-            for c in range(BLOCKS):
-                nc.scalar.activation(
-                    scaled[r][:, c, :], bank[5 + r][:, c * P : (c + 1) * P], ACT.Copy, scale=gate_cols[r][:, c : c + 1]
-                )
-        for r in range(TOP - 1):
-            for c in range(BLOCKS):
+        turned = {}
+        for h, (c0, c1) in enumerate(TURNED_PIECES):
+            for r in range(TOP - 1):
+                nc.scalar.activation(picked[c0, r][:], results(r + 1, c0 * P, c1 * P), ACT.Copy)
+                for c in range(c0, c1):
+                    turned[c, r] = bank[BLOCKS + 2 * h + r][:, (c - c0) * P : (c - c0 + 1) * P]
+                    nc.tensor.transpose(turned[c, r], picked[c0, r][:, (c - c0) * P : (c - c0 + 1) * P], ident[:])
+        rest_picked = [
+            held.tile([P, c1 - c0], F32, name=f"rest_picked{c0}", tag=tag)
+            for (c0, c1), tag in zip(REST_PIECES, ("rest_picked", "picked2_1"))
+        ]
+
+        def pick_rest(h):
+            c0, c1 = REST_PIECES[h]
+            nc.scalar.activation(rest_picked[h][:], results(TOP - 1, TURNED + c0, TURNED + c1), ACT.Copy)
+
+        pick_rest(0)
+        for c in range(BLOCKS):
+            for r in range(TOP - 1):
+                nc.scalar.activation(scaled[r][:, c, :], turned[c, r], ACT.Copy, scale=gate_cols[r][:, c : c + 1])
                 nc.tensor.matmul(
                     bank[c][:, 0:P], scaled[r][:, c, :], ident[:], start=(r == 0), stop=(r == TOP - 2), is_transpose=True
                 )
-        rest_picked = [
-            held.tile([P, c1 - c0], F32, name=f"rest_picked{c0}", tag=tag)
-            for (c0, c1), tag in zip(REST_PIECES, ("rest_picked", "picked1"))
-        ]
-        for h, (c0, c1) in enumerate(REST_PIECES):
-            nc.scalar.activation(rest_picked[h][:], results(TOP - 1, TURNED + c0, TURNED + c1), ACT.Copy)
+        pick_rest(1)
 
         for r in range(TOP - 1):
             nc.vector.tensor_tensor(rest_gated[r][:], results(r, TURNED, T), rest_gate(r), ALU.mult)

@@ -41,7 +41,7 @@ EARLY_EXPERTS = 5
 EARLY = EARLY_EXPERTS * C
 SCALE_WINDOW = 2048
 LAST = (E - 1) * C
-SQUARE = 2 * C
+SQUARE = 3 * C
 
 BLOCKS = 3
 TURNED = BLOCKS * P
@@ -166,7 +166,7 @@ def tile_moe_tk_lin_relu2_kernel(
             for t0, t1 in ROUNDS[step]:
                 nc.scalar.activation(*round_views(step, t0, t1), ACT.Copy)
 
-        for step, cut, stop in ((0, LONG, SLOTS), (1, LONG, SLOTS), (2, EARLY - C, EARLY)):
+        for step, cut, stop in ((0, LONG, SLOTS), (1, LONG, SLOTS), (2, EARLY - P, EARLY)):
             new_words(step, 0, cut)
             gather_words(step, 0, cut)
             for t0, t1 in QUANT[step + 1]:
@@ -191,7 +191,7 @@ def tile_moe_tk_lin_relu2_kernel(
                 return bank[s0 // C][:, s0 % C : s0 % C + s1 - s0]
             if s0 < LAST:
                 return bank[(s0 - EARLY) // C][:, C + s0 % C : C + s0 % C + s1 - s0]
-            return bank[(LAST - EARLY) // C + (s0 - LAST) // P][:, C : C + P]
+            return bank[(s0 - LAST) // P][:, 0:P]
 
         def multiply(step, s0, s1):
             matrix = 2 * (s0 // C) + ORDER[step] % 2
@@ -207,9 +207,8 @@ def tile_moe_tk_lin_relu2_kernel(
             )
 
         def multiply_narrow(step, s0, s1):
-            width = C if s0 < LAST else P
-            for g0 in range(s0, s1, width):
-                multiply(step, g0, g0 + width)
+            for g0 in range(s0, s1, P):
+                multiply(step, g0, g0 + P)
 
         def step_2(s0, s1):
             gather_words(2, s0, s1)
@@ -250,10 +249,10 @@ def tile_moe_tk_lin_relu2_kernel(
             multiply_narrow(2, s0, s1)
             step_3(s0, s1)
         open_sums(EARLY_EXPERTS, E - 1)
-        multiply_narrow(0, LAST, SLOTS)
-        multiply_narrow(1, LAST, SLOTS)
         step_2(EARLY, LAST)
         step_3(EARLY, LAST - C)
+        multiply_narrow(0, LAST, SLOTS)
+        multiply_narrow(1, LAST, SLOTS)
         step_3(LAST - C, LAST)
         step_2(LAST, SLOTS)
         step_3_last(LAST, P)

@@ -23,8 +23,8 @@ TOP = 3
 STEPS = 4
 QUADRANTS = 4
 
-ORDER = (0, 2, 3, 1)
-PLANE = (4, 0, 12, 8)
+ORDER = (2, 0, 3, 1)
+PLANE = (0, 4, 12, 8)
 MOVED = 2
 W8_PLANE = 8
 
@@ -33,9 +33,9 @@ THIRDS = ((0, 256), (256, 512), (512, 768))
 WIDE = ((0, 512), (512, 768))
 LOADS = (HEAD, THIRDS, ((0, T),), ((0, T),))
 ROUNDS = (HEAD, THIRDS, WIDE, WIDE)
-QUANT = (HEAD, WIDE, WIDE, WIDE)
+QUANT = (HEAD[:-1] + ((640, 704), (704, 768)), WIDE, WIDE, WIDE)
 
-WINDOWS = ((3 * T // 4, T), (3 * T // 2, 2 * T), (2048, 4096))
+WINDOWS = ((3 * T // 4, T), (3 * T // 2, 2 * T), (1536, 2048), (2048, 4096))
 LONG, WIDEST = WINDOWS[-1]
 EARLY_EXPERTS = 5
 EARLY = EARLY_EXPERTS * C
@@ -81,7 +81,7 @@ def tile_moe_tk_lin_relu2_kernel(
         b_t = held.tile([P, E], F32, name="b_t")
         relu_t = held.tile([P, SLOTS], F32, name="relu_t")
         y_t = held.tile([P, SLOTS], F32, name="y_t")
-        ident = held.tile([P, P], F32, name="ident")
+        ident = held.tile([P, P], F32, name="ident", tag=f"x_b0_{QUANT[0][-1][0]}", align_bytes=64)
         gate_cols = [held.tile([P, BLOCKS], F32, name=f"gate_cols{r}") for r in range(TOP - 1)]
         fused = held.tile([P, TURNED], F32, name="fused")
         picked = {
@@ -95,7 +95,6 @@ def tile_moe_tk_lin_relu2_kernel(
         out_t = held.tile([P, T], F32, name="out_t")
         bank = [psum.tile([P, 512], F32, name=f"bank{i}") for i in range(BANKS)]
 
-        make_identity(nc, ident[:])
         nc.vector.memset(x_scales[:, 0:T].bitcast(I32), 0)
         nc.vector.memset(w_scales[:].rearrange("p g n -> p (g n)").bitcast(I32), 0)
         nc.vector.memset(moved_scales[:].bitcast(I32), 0)
@@ -161,12 +160,15 @@ def tile_moe_tk_lin_relu2_kernel(
             cut = (t0 + t1) // 2
             nc.scalar.activation(*round_views(0, cut, t1), ACT.Copy)
             nc.vector.tensor_copy(*round_views(0, t0, cut))
-            quantise(0, t0, t1)
+            for q0, q1 in QUANT[0]:
+                if t0 <= q0 < t1:
+                    quantise(0, q0, q1)
+        make_identity(nc, ident[:])
         for step in range(1, STEPS):
             for t0, t1 in ROUNDS[step]:
                 nc.scalar.activation(*round_views(step, t0, t1), ACT.Copy)
 
-        for step, cut, stop in ((0, LONG, SLOTS), (1, LONG, SLOTS), (2, EARLY - P, EARLY)):
+        for step, cut, stop in ((0, LONG, SLOTS), (1, LONG, SLOTS), (2, EARLY - C, EARLY)):
             new_words(step, 0, cut)
             gather_words(step, 0, cut)
             for t0, t1 in QUANT[step + 1]:
@@ -206,13 +208,13 @@ def tile_moe_tk_lin_relu2_kernel(
                 stop=(step == STEPS - 1),
             )
 
-        def multiply_narrow(step, s0, s1):
-            for g0 in range(s0, s1, P):
-                multiply(step, g0, g0 + P)
+        def multiply_experts(step, s0, s1):
+            for g0 in range(s0, s1, C):
+                multiply(step, g0, g0 + C)
 
-        def step_2(s0, s1):
-            gather_words(2, s0, s1)
-            multiply_narrow(2, s0, s1)
+        def multiply_halves(step):
+            for g0 in range(LAST, SLOTS, P):
+                multiply(step, g0, g0 + P)
 
         def step_3(s0, s1):
             gather_words(3, s0, s1)
@@ -235,7 +237,7 @@ def tile_moe_tk_lin_relu2_kernel(
         def open_sums(e0, e1):
             for e in range(e0, e1):
                 multiply(0, e * C, (e + 1) * C)
-                multiply_narrow(1, e * C, (e + 1) * C)
+                multiply(1, e * C, (e + 1) * C)
 
         gather_scales(0, EARLY)
         open_sums(0, EARLY_EXPERTS)
@@ -246,15 +248,17 @@ def tile_moe_tk_lin_relu2_kernel(
             out=gate_t[:, T:].rearrange("p (r t) -> p r t", r=2), in_=gate[1:TOP, :, TURNED:T].rearrange("r p t -> p r t")
         )
         for s0, s1 in ((0, 2 * C), (2 * C, EARLY)):
-            multiply_narrow(2, s0, s1)
+            multiply_experts(2, s0, s1)
             step_3(s0, s1)
         open_sums(EARLY_EXPERTS, E - 1)
-        step_2(EARLY, LAST)
+        gather_words(2, EARLY, LAST)
+        multiply_experts(2, EARLY, LAST)
         step_3(EARLY, LAST - C)
-        multiply_narrow(0, LAST, SLOTS)
-        multiply_narrow(1, LAST, SLOTS)
+        multiply_halves(0)
+        multiply_halves(1)
         step_3(LAST - C, LAST)
-        step_2(LAST, SLOTS)
+        gather_words(2, LAST, SLOTS)
+        multiply_halves(2)
         step_3_last(LAST, P)
         step_3_last(LAST + P, P // 2)
 

@@ -31,7 +31,7 @@ W8_PLANE = 8
 HEAD = ((0, 256), (256, 512), (512, 640), (640, 768))
 THIRDS = ((0, 256), (256, 512), (512, 768))
 WIDE = ((0, 512), (512, 768))
-LOADS = (HEAD, THIRDS, ((0, T),), ((0, T),))
+LOADS = (HEAD, THIRDS, WIDE, WIDE)
 ROUNDS = (HEAD, THIRDS, WIDE, WIDE)
 QUANT = (HEAD[:-1] + ((640, 704), (704, 768)), WIDE, WIDE, WIDE)
 
@@ -115,8 +115,11 @@ def tile_moe_tk_lin_relu2_kernel(
                     out=w_scales[32 * q + first : 32 * q + first + 4].bitcast(I32),
                     in_=scales[:, :, 4 * q : 4 * q + 4, :].rearrange("e a q n -> q (e a) n").bitcast(I32),
                 )
-        nc.sync.dma_start(out=w8_t[:].bitcast(I32), in_=w8_words.rearrange("e a p n r -> p (e a) (n r)").bitcast(I32))
-        nc.sync.dma_start(out=w4_t[:].bitcast(I32), in_=w4_words.rearrange("e a p n -> p (e a) n").bitcast(I32))
+        w8_rows = w8_words.rearrange("e a p n r -> p (e a) (n r)").bitcast(I32)
+        w4_rows = w4_words.rearrange("e a p n -> p (e a) n").bitcast(I32)
+        for m0, m1 in ((0, 2 * EARLY_EXPERTS), (2 * EARLY_EXPERTS, 2 * E)):
+            nc.sync.dma_start(out=w4_t[:, m0:m1, :].bitcast(I32), in_=w4_rows[:, m0:m1, :])
+            nc.sync.dma_start(out=w8_t[:, m0:m1, :].bitcast(I32), in_=w8_rows[:, m0:m1, :])
         nc.sync.dma_start(out=b_t[:], in_=b)
         for pos_tile, pos in zip(pos_t, (pos1, pos2, pos3)):
             nc.sync.dma_start(pos_tile[:], pos)
@@ -168,24 +171,24 @@ def tile_moe_tk_lin_relu2_kernel(
             for t0, t1 in ROUNDS[step]:
                 nc.scalar.activation(*round_views(step, t0, t1), ACT.Copy)
 
-        for step, cut, stop in ((0, LONG, SLOTS), (1, LONG, SLOTS), (2, EARLY - C, EARLY)):
-            new_words(step, 0, cut)
-            gather_words(step, 0, cut)
-            for t0, t1 in QUANT[step + 1]:
-                quantise(step + 1, t0, t1)
-            new_words(step, cut, stop, tag=f"x_f{step + 1}_{LOADS[step + 1][-1][0]}")
-            gather_words(step, cut, stop)
+        for step, later in ((0, (1,)), (1, (2, 3))):
+            new_words(step, 0, LONG)
+            gather_words(step, 0, LONG)
+            for nxt in later:
+                for t0, t1 in QUANT[nxt]:
+                    quantise(nxt, t0, t1)
+            new_words(step, LONG, SLOTS, tag=f"x_f{later[-1]}_{LOADS[later[-1]][-1][0]}")
+            gather_words(step, LONG, SLOTS)
 
-        def gather_scales(s0, s1):
+        for s0, s1 in ((0, EARLY), (EARLY, SLOTS)):
             nc.vector.tensor_copy(slot_scales[:, s0:s1], x_scales[:].indirect(offs_t[:, s0 // 16 : s1 // 16]))
-            for q in range(QUADRANTS):
-                row = 32 * q + PLANE[MOVED]
-                nc.sync.dma_start(
-                    out=moved_scales[32 * q : 32 * q + 4, s0:s1].bitcast(I32),
-                    in_=slot_scales[row : row + 4, s0:s1].bitcast(I32),
-                )
+        for q in range(QUADRANTS):
+            row = 32 * q + PLANE[MOVED]
+            nc.sync.dma_start(
+                out=moved_scales[32 * q : 32 * q + 4, :].bitcast(I32), in_=slot_scales[row : row + 4, :].bitcast(I32)
+            )
 
-        new_words(2, EARLY, SLOTS, tag=f"x_b3_{QUANT[3][-1][0]}")
+        new_words(2, 0, SLOTS, tag=f"x_b3_{QUANT[3][-1][0]}")
         new_words(3, 0, SLOTS)
 
         def sums(s0, s1):
@@ -239,14 +242,13 @@ def tile_moe_tk_lin_relu2_kernel(
                 multiply(0, e * C, (e + 1) * C)
                 multiply(1, e * C, (e + 1) * C)
 
-        gather_scales(0, EARLY)
         open_sums(0, EARLY_EXPERTS)
-        gather_scales(EARLY, SLOTS)
         gate_t = held.tile([P, T + 2 * REST], F32, name="gate_t", tag="x_scales", align_bytes=64)
         nc.sync.dma_start(out=gate_t[:, 0:T], in_=gate[0])
         nc.sync.dma_start(
             out=gate_t[:, T:].rearrange("p (r t) -> p r t", r=2), in_=gate[1:TOP, :, TURNED:T].rearrange("r p t -> p r t")
         )
+        gather_words(2, 0, EARLY)
         for s0, s1 in ((0, 2 * C), (2 * C, EARLY)):
             multiply_experts(2, s0, s1)
             step_3(s0, s1)

@@ -130,8 +130,8 @@ def tile_moe_tk_lin_relu2_kernel(
         def round_views(step, t0, t1):
             f0 = max(lo for lo, hi in LOADS[step] if lo <= t0)
             b0 = max(lo for lo, hi in QUANT[step] if lo <= t0)
-            src = x_f[step, f0][:, :, t0 - f0 : t1 - f0].rearrange("p j (c i) -> p c j i", i=4)
-            dst = x_b[step, b0][:, t0 - b0 : t1 - b0, :].rearrange("p (c i) j -> p c j i", i=4)
+            src = x_f[step, f0][:, :, t0 - f0 : t1 - f0].rearrange("p j (c i) -> p c j i", i=2)
+            dst = x_b[step, b0][:, t0 - b0 : t1 - b0, :].rearrange("p (c i) j -> p c j i", i=2)
             return dst, src
 
         def first_word(step):

@@ -31,8 +31,8 @@ W8_PLANE = 8
 HEAD = ((0, 256), (256, 512), (512, 640), (640, 768))
 THIRDS = ((0, 256), (256, 512), (512, 768))
 WIDE = ((0, 512), (512, 768))
-LOADS = (HEAD, THIRDS, WIDE, WIDE)
-ROUNDS = (HEAD, THIRDS, WIDE, WIDE)
+LOADS = (HEAD, THIRDS, WIDE, THIRDS)
+ROUNDS = LOADS
 QUANT = (HEAD[:-1] + ((640, 704), (704, 768)), WIDE, WIDE, WIDE)
 
 WINDOWS = ((3 * T // 4, T), (3 * T // 2, 2 * T), (1536, 2048), (2048, 4096))
@@ -116,9 +116,8 @@ def tile_moe_tk_lin_relu2_kernel(
                     in_=scales[:, :, 4 * q : 4 * q + 4, :].rearrange("e a q n -> q (e a) n").bitcast(I32),
                 )
         w8_rows = w8_words.rearrange("e a p n r -> p (e a) (n r)").bitcast(I32)
-        w4_rows = w4_words.rearrange("e a p n -> p (e a) n").bitcast(I32)
+        nc.sync.dma_start(out=w4_t[:].bitcast(I32), in_=w4_words.rearrange("e a p n -> p (e a) n").bitcast(I32))
         for m0, m1 in ((0, 2 * EARLY_EXPERTS), (2 * EARLY_EXPERTS, 2 * E)):
-            nc.sync.dma_start(out=w4_t[:, m0:m1, :].bitcast(I32), in_=w4_rows[:, m0:m1, :])
             nc.sync.dma_start(out=w8_t[:, m0:m1, :].bitcast(I32), in_=w8_rows[:, m0:m1, :])
         nc.sync.dma_start(out=b_t[:], in_=b)
         for pos_tile, pos in zip(pos_t, (pos1, pos2, pos3)):
@@ -235,7 +234,10 @@ def tile_moe_tk_lin_relu2_kernel(
             for q0 in range(0, P, width):
                 cols, half_sums = slice(s0 + q0, s0 + q0 + width), sums(s0, s0 + P)[:, q0 : q0 + width]
                 nc.vector.tensor_scalar(relu_t[:, cols], half_sums, b_t[:, E - 1 : E], 0.0, ALU.add, ALU.max)
-                nc.scalar.activation(y_t[:, cols], relu_t[:, cols], ACT.Square)
+                if s0 == LAST:
+                    nc.vector.tensor_tensor(y_t[:, cols], relu_t[:, cols], relu_t[:, cols], ALU.mult)
+                else:
+                    nc.scalar.activation(y_t[:, cols], relu_t[:, cols], ACT.Square)
 
         def open_sums(e0, e1):
             for e in range(e0, e1):

@@ -195,7 +195,7 @@ def tile_moe_tk_lin_relu2_kernel(
                 return bank[s0 // C][:, s0 % C : s0 % C + s1 - s0]
             if s0 < LAST:
                 return bank[(s0 - EARLY) // C][:, C + s0 % C : C + s0 % C + s1 - s0]
-            return bank[(s0 - LAST) // P][:, 0:P]
+            return bank[3 + (s0 - LAST) // P][:, C : C + P]
 
         def multiply(step, s0, s1):
             matrix = 2 * (s0 // C) + ORDER[step] % 2
@@ -218,14 +218,12 @@ def tile_moe_tk_lin_relu2_kernel(
             for g0 in range(LAST, SLOTS, P):
                 multiply(step, g0, g0 + P)
 
-        def step_3(s0, s1):
-            gather_words(3, s0, s1)
+        def activate(s0, s1, widest):
             for e in range(s0 // C, s1 // C):
                 cols = slice(e * C, (e + 1) * C)
-                multiply(3, e * C, (e + 1) * C)
                 nc.scalar.activation(relu_t[:, cols], sums(e * C, (e + 1) * C), ACT.Relu, bias=b_t[:, e : e + 1])
-            for q0 in range(s0, s1, SQUARE):
-                q1 = min(q0 + SQUARE, s1)
+            for q0 in range(s0, s1, widest):
+                q1 = min(q0 + widest, s1)
                 nc.scalar.activation(y_t[:, q0:q1], relu_t[:, q0:q1], ACT.Square)
 
         def step_3_last(s0, width):
@@ -251,20 +249,36 @@ def tile_moe_tk_lin_relu2_kernel(
             out=gate_t[:, T:].rearrange("p (r t) -> p r t", r=2), in_=gate[1:TOP, :, TURNED:T].rearrange("r p t -> p r t")
         )
         gather_words(2, 0, EARLY)
-        for s0, s1 in ((0, 2 * C), (2 * C, EARLY)):
-            multiply_experts(2, s0, s1)
-            step_3(s0, s1)
+        multiply_experts(2, 0, EARLY)
+        gather_words(3, 0, EARLY)
+        multiply_experts(3, 0, EARLY)
+        activate(0, EARLY, SQUARE)
         open_sums(EARLY_EXPERTS, E - 1)
-        gather_words(2, EARLY, LAST)
-        multiply_experts(2, EARLY, LAST)
-        step_3(EARLY, LAST - C)
         multiply_halves(0)
         multiply_halves(1)
-        step_3(LAST - C, LAST)
+        gather_words(2, EARLY, LAST)
+        multiply_experts(2, EARLY, LAST)
+        gather_words(3, EARLY, LAST)
+        multiply_experts(3, EARLY, LAST)
+        activate(EARLY, LAST - C, C)
         gather_words(2, LAST, SLOTS)
         multiply_halves(2)
-        step_3_last(LAST, P)
-        step_3_last(LAST + P, P // 2)
+        for s0 in (LAST, LAST + P):
+            gather_words(3, s0, s0 + P)
+            multiply(3, s0, s0 + P)
+
+        def relu_on_vector(s0, q0, q1, width):
+            cols, e = slice(s0 + q0, s0 + q1), s0 // C
+            nc.vector.tensor_scalar(relu_t[:, cols], sums(s0, s0 + width)[:, q0:q1], b_t[:, e : e + 1], 0.0, ALU.add, ALU.max)
+            return cols
+
+        cols = relu_on_vector(LAST - C, 0, C, C)
+        nc.scalar.activation(y_t[:, cols], relu_t[:, cols], ACT.Square)
+        first_half = relu_on_vector(LAST, 0, P, P)
+        for q0 in range(0, P, P // 2):
+            cols = relu_on_vector(LAST + P, q0, q0 + P // 2, P)
+            nc.scalar.activation(y_t[:, cols], relu_t[:, cols], ACT.Square)
+        nc.vector.tensor_tensor(y_t[:, first_half], relu_t[:, first_half], relu_t[:, first_half], ALU.mult)
 
         def results(r, t0, t1):
             return y_t[:].indirect(pos_t[r][:, t0 // 16 : t1 // 16])

@@ -272,9 +272,11 @@ def tile_moe_tk_lin_relu2_kernel(
             nc.vector.tensor_scalar(relu_t[:, cols], sums(s0, s0 + width)[:, q0:q1], b_t[:, e : e + 1], 0.0, ALU.add, ALU.max)
             return cols
 
-        cols = relu_on_vector(LAST - C, 0, C, C)
+        relu_on_vector(LAST - C, 0, C, C)
+        cols = slice(LAST - C, LAST - P)
         nc.scalar.activation(y_t[:, cols], relu_t[:, cols], ACT.Square)
-        first_half = relu_on_vector(LAST, 0, P, P)
+        relu_on_vector(LAST, 0, P, P)
+        first_half = slice(LAST - P, LAST + P)
         for q0 in range(0, P, P // 2):
             cols = relu_on_vector(LAST + P, q0, q0 + P // 2, P)
             nc.scalar.activation(y_t[:, cols], relu_t[:, cols], ACT.Square)

from contextlib import ExitStack

import concourse.mybir as mybir
from concourse.masks import make_identity

K, T, E, C, N = 2048, 768, 9, 256, 128
SLOTS = E * C
FLOPS = 2 * K * N * SLOTS

F32 = mybir.dt.float32
BF16 = mybir.dt.bfloat16
I32 = mybir.dt.int32
U32 = mybir.dt.uint32
U16 = mybir.dt.uint16
U8 = mybir.dt.uint8
FP8X4 = mybir.dt.float8_e4m3fn_x4
FP4X4 = mybir.dt.float4_e2m1fn_x4
ACT = mybir.ActivationFunctionType
ALU = mybir.AluOpType

P = 128
TOP = 3
STEPS = 4
QUADRANTS = 4

ORDER = (2, 0, 3, 1)
PLANE = (0, 4, 12, 8)
MOVED = 2
W8_PLANE = 8

HEAD = ((0, 256), (256, 512), (512, 640), (640, 768))
THIRDS = ((0, 256), (256, 512), (512, 768))
WIDE = ((0, 512), (512, 768))
LOADS = (HEAD, THIRDS, WIDE, THIRDS)
ROUNDS = LOADS
QUANT = (HEAD[:-1] + ((640, 704), (704, 768)), WIDE, WIDE, WIDE)

WINDOWS = ((3 * T // 4, T), (3 * T // 2, 2 * T), (1536, 2048), (2048, 4096))
LONG, WIDEST = WINDOWS[-1]
EARLY_EXPERTS = 5
EARLY = EARLY_EXPERTS * C
SCALE_WINDOW = 2048
LAST = (E - 1) * C
SQUARE = 3 * C

BLOCKS = 3
TURNED = BLOCKS * P
REST = T - TURNED
TURNED_PIECES = ((0, 2), (2, 3))
REST_PIECES = ((0, 256), (256, 384))
BANKS = 8


def tile_moe_tk_lin_relu2_kernel(
    tc, xT, w8_words, w8_scales, w4_words, w4_scales, b, gate, offs, pos1, pos2, pos3, out
):
    nc = tc.nc
    with ExitStack() as ctx:
        held = ctx.enter_context(tc.tile_pool(name="held", bufs=1))
        psum = ctx.enter_context(tc.psum_pool(name="psum", bufs=1))

        offs_t = held.tile([P, SLOTS // 16], U16, name="offs_t")
        pos_t = [held.tile([P, T // 16], U16, name=f"pos_t{r}") for r in range(TOP)]
        x_f = {
            (step, t0): held.tile([P, 4, t1 - t0], F32, name=f"x_f{step}_{t0}", align_bytes=64)
            for step in range(STEPS)
            for t0, t1 in LOADS[step]
        }
        x_b = {
            (step, t0): held.tile([P, t1 - t0, 4], BF16, name=f"x_b{step}_{t0}", align_bytes=64)
            for step in range(STEPS)
            for t0, t1 in QUANT[step]
        }
        x_words = held.tile([P, (STEPS - 1) * T + WIDEST], I32, name="x_words", align_bytes=64)
        x_scales = held.tile([P, SCALE_WINDOW], U8, name="x_scales", tag="x_scales", align_bytes=64)
        slot_scales = held.tile([P, SLOTS], U8, name="slot_scales", align_bytes=64)
        moved_scales = held.tile([P, SLOTS], U8, name="moved_scales", align_bytes=64)
        w8_t = held.tile([P, 2 * E, 4 * N], U8, name="w8_t", align_bytes=64)
        w4_t = held.tile([P, 2 * E, 2 * N], U8, name="w4_t", align_bytes=64)
        w_scales = held.tile([P, 2 * E, N], U8, name="w_scales", align_bytes=64)
        b_t = held.tile([P, E], F32, name="b_t")
        relu_t = held.tile([P, SLOTS], F32, name="relu_t")
        y_t = held.tile([P, SLOTS], F32, name="y_t")
        ident = held.tile([P, P], F32, name="ident", tag=f"x_b0_{QUANT[0][-1][0]}", align_bytes=64)
        gate_cols = [held.tile([P, BLOCKS], F32, name=f"gate_cols{r}") for r in range(TOP - 1)]
        fused = held.tile([P, TURNED], F32, name="fused")
        picked = {
            (c0, r): held.tile([P, (c1 - c0) * P], F32, name=f"picked{c0}_{r}")
            for c0, c1 in TURNED_PIECES
            for r in range(TOP - 1)
        }
        scaled = [held.tile([P, BLOCKS, P], F32, name=f"scaled{r}") for r in range(TOP - 1)]
        rest_gated = [held.tile([P, w], F32, name=f"rest_gated{r}") for r, w in enumerate((REST, REST, REST))]
        rest_pair = held.tile([P, REST], F32, name="rest_pair")
        out_t = held.tile([P, T], F32, name="out_t")
        bank = [psum.tile([P, 512], F32, name=f"bank{i}") for i in range(BANKS)]

        nc.vector.memset(x_scales[:, 0:T].bitcast(I32), 0)
        nc.vector.memset(w_scales[:].rearrange("p g n -> p (g n)").bitcast(I32), 0)
        nc.vector.memset(moved_scales[:].bitcast(I32), 0)

        x_rows = xT.rearrange("(a p j) t -> a p j t", a=STEPS, j=4)

        def load_x(step):
            for t0, t1 in LOADS[step]:
                nc.sync.dma_start(out=x_f[step, t0][:], in_=x_rows[ORDER[step], :, :, t0:t1])

        load_x(0)
        nc.sync.dma_start(offs_t[:], offs)
        for step in range(1, STEPS):
            load_x(step)
        for first, scales in ((W8_PLANE, w8_scales), (0, w4_scales)):
            for q in range(QUADRANTS):
                nc.sync.dma_start(
                    out=w_scales[32 * q + first : 32 * q + first + 4].bitcast(I32),
                    in_=scales[:, :, 4 * q : 4 * q + 4, :].rearrange("e a q n -> q (e a) n").bitcast(I32),
                )
        w8_rows = w8_words.rearrange("e a p n r -> p (e a) (n r)").bitcast(I32)
        nc.sync.dma_start(out=w4_t[:].bitcast(I32), in_=w4_words.rearrange("e a p n -> p (e a) n").bitcast(I32))
        for m0, m1 in ((0, 2 * EARLY_EXPERTS), (2 * EARLY_EXPERTS, 2 * E)):
            nc.sync.dma_start(out=w8_t[:, m0:m1, :].bitcast(I32), in_=w8_rows[:, m0:m1, :])
        nc.sync.dma_start(out=b_t[:], in_=b)
        for pos_tile, pos in zip(pos_t, (pos1, pos2, pos3)):
            nc.sync.dma_start(pos_tile[:], pos)
        with nc.allow_non_contiguous_dma(reason="one gate value a partition"):
            for r in range(TOP - 1):
                nc.sync.dma_start(out=gate_cols[r][:], in_=gate[r + 1, 0, 0:TURNED].rearrange("(c p) -> p c", p=P))

        def round_views(step, t0, t1):
            f0 = max(lo for lo, hi in LOADS[step] if lo <= t0)
            b0 = max(lo for lo, hi in QUANT[step] if lo <= t0)
            src = x_f[step, f0][:, :, t0 - f0 : t1 - f0].rearrange("p j (c i) -> p c j i", i=2)
            dst = x_b[step, b0][:, t0 - b0 : t1 - b0, :].rearrange("p (c i) j -> p c j i", i=2)
            return dst, src

        def first_word(step):
            return (STEPS - 1 - step) * T

        def quantise(step, t0, t1):
            nc.vector.quantize_mx(
                out=x_words[:, first_word(step) + t0 : first_word(step) + t1].bitcast(FP8X4),
                scales=x_scales[PLANE[step] : P, t0:t1],
                in_=x_b[step, t0][:].rearrange("p t j -> p (t j)"),
            )

        slot_words = {}

        def new_words(step, s0, s1, tag=None):
            name = f"slot_words{step}_{s0}"
            slot_words[step, s0] = held.tile([P, s1 - s0], U32, name=name, tag=tag or name, align_bytes=64)

        def words(step, s0, s1):
            lo = max(first for of_step, first in slot_words if of_step == step and first <= s0)
            return slot_words[step, lo][:, s0 - lo : s1 - lo]

        def gather_words(step, s0, s1):
            width = min(columns for longest, columns in WINDOWS if s1 - s0 <= longest)
            window = x_words[:, first_word(step) : first_word(step) + width].bitcast(U32)
            nc.vector.tensor_copy(words(step, s0, s1), window.indirect(offs_t[:, s0 // 16 : s1 // 16]))

        for t0, t1 in ROUNDS[0]:
            cut = (t0 + t1) // 2
            nc.scalar.activation(*round_views(0, cut, t1), ACT.Copy)
            nc.vector.tensor_copy(*round_views(0, t0, cut))
            for q0, q1 in QUANT[0]:
                if t0 <= q0 < t1:
                    quantise(0, q0, q1)
        make_identity(nc, ident[:])
        for step in range(1, STEPS):
            for t0, t1 in ROUNDS[step]:
                nc.scalar.activation(*round_views(step, t0, t1), ACT.Copy)

        for step, later in ((0, (1,)), (1, (2, 3))):
            new_words(step, 0, LONG)
            gather_words(step, 0, LONG)
            for nxt in later:
                for t0, t1 in QUANT[nxt]:
                    quantise(nxt, t0, t1)
            new_words(step, LONG, SLOTS, tag=f"x_f{later[-1]}_{LOADS[later[-1]][-1][0]}")
            gather_words(step, LONG, SLOTS)

        for s0, s1 in ((0, EARLY), (EARLY, SLOTS)):
            nc.vector.tensor_copy(slot_scales[:, s0:s1], x_scales[:].indirect(offs_t[:, s0 // 16 : s1 // 16]))
        for q in range(QUADRANTS):
            row = 32 * q + PLANE[MOVED]
            nc.sync.dma_start(
                out=moved_scales[32 * q : 32 * q + 4, :].bitcast(I32), in_=slot_scales[row : row + 4, :].bitcast(I32)
            )

        new_words(2, 0, SLOTS, tag=f"x_b3_{QUANT[3][-1][0]}")
        new_words(3, 0, SLOTS)

        def sums(s0, s1):
            if s0 < EARLY:
                return bank[s0 // C][:, s0 % C : s0 % C + s1 - s0]
            if s0 < LAST:
                return bank[(s0 - EARLY) // C][:, C + s0 % C : C + s0 % C + s1 - s0]
            return bank[3 + (s0 - LAST) // P][:, C : C + P]

        def multiply(step, s0, s1):
            matrix = 2 * (s0 // C) + ORDER[step] % 2
            is_fp8 = ORDER[step] < 2
            nc.tensor.matmul_mx(
                out=sums(s0, s1),
                lhsT=w8_t[:, matrix, :].bitcast(FP8X4) if is_fp8 else w4_t[:, matrix, :].bitcast(FP4X4),
                lhsT_scale=w_scales[(W8_PLANE if is_fp8 else 0) : P, matrix, :],
                rhs=words(step, s0, s1).bitcast(FP8X4),
                rhs_scale=moved_scales[:, s0:s1] if step == MOVED else slot_scales[PLANE[step] : P, s0:s1],
                start=(step == 0),
                stop=(step == STEPS - 1),
            )

        def multiply_experts(step, s0, s1):
            for g0 in range(s0, s1, C):
                multiply(step, g0, g0 + C)

        def multiply_halves(step):
            for g0 in range(LAST, SLOTS, P):
                multiply(step, g0, g0 + P)

        def activate(s0, s1, widest):
            for e in range(s0 // C, s1 // C):
                cols = slice(e * C, (e + 1) * C)
                nc.scalar.activation(relu_t[:, cols], sums(e * C, (e + 1) * C), ACT.Relu, bias=b_t[:, e : e + 1])
            for q0 in range(s0, s1, widest):
                q1 = min(q0 + widest, s1)
                nc.scalar.activation(y_t[:, q0:q1], relu_t[:, q0:q1], ACT.Square)

        def step_3_last(s0, width):
            gather_words(3, s0, s0 + P)
            multiply(3, s0, s0 + P)
            for q0 in range(0, P, width):
                cols, half_sums = slice(s0 + q0, s0 + q0 + width), sums(s0, s0 + P)[:, q0 : q0 + width]
                nc.vector.tensor_scalar(relu_t[:, cols], half_sums, b_t[:, E - 1 : E], 0.0, ALU.add, ALU.max)
                if s0 == LAST:
                    nc.vector.tensor_tensor(y_t[:, cols], relu_t[:, cols], relu_t[:, cols], ALU.mult)
                else:
                    nc.scalar.activation(y_t[:, cols], relu_t[:, cols], ACT.Square)

        def open_sums(e0, e1):
            for e in range(e0, e1):
                multiply(0, e * C, (e + 1) * C)
                multiply(1, e * C, (e + 1) * C)

        open_sums(0, EARLY_EXPERTS)
        gate_t = held.tile([P, T + 2 * REST], F32, name="gate_t", tag="x_scales", align_bytes=64)
        nc.sync.dma_start(out=gate_t[:, 0:T], in_=gate[0])
        nc.sync.dma_start(
            out=gate_t[:, T:].rearrange("p (r t) -> p r t", r=2), in_=gate[1:TOP, :, TURNED:T].rearrange("r p t -> p r t")
        )
        gather_words(2, 0, EARLY)
        multiply_experts(2, 0, EARLY)
        gather_words(3, 0, EARLY)
        multiply_experts(3, 0, EARLY)
        activate(0, EARLY, SQUARE)
        open_sums(EARLY_EXPERTS, E - 1)
        multiply_halves(0)
        multiply_halves(1)
        gather_words(2, EARLY, LAST)
        multiply_experts(2, EARLY, LAST)
        gather_words(3, EARLY, LAST)
        multiply_experts(3, EARLY, LAST)
        activate(EARLY, LAST - C, C)
        gather_words(2, LAST, SLOTS)
        multiply_halves(2)
        for s0 in (LAST, LAST + P):
            gather_words(3, s0, s0 + P)
            multiply(3, s0, s0 + P)

        def relu_on_vector(s0, q0, q1, width):
            cols, e = slice(s0 + q0, s0 + q1), s0 // C
            nc.vector.tensor_scalar(relu_t[:, cols], sums(s0, s0 + width)[:, q0:q1], b_t[:, e : e + 1], 0.0, ALU.add, ALU.max)
            return cols

        relu_on_vector(LAST - C, 0, C, C)
        cols = slice(LAST - C, LAST - P)
        nc.scalar.activation(y_t[:, cols], relu_t[:, cols], ACT.Square)
        relu_on_vector(LAST, 0, P, P)
        first_half = slice(LAST - P, LAST + P)
        for q0 in range(0, P, P // 2):
            cols = relu_on_vector(LAST + P, q0, q0 + P // 2, P)
            nc.scalar.activation(y_t[:, cols], relu_t[:, cols], ACT.Square)
        nc.vector.tensor_tensor(y_t[:, first_half], relu_t[:, first_half], relu_t[:, first_half], ALU.mult)

        def results(r, t0, t1):
            return y_t[:].indirect(pos_t[r][:, t0 // 16 : t1 // 16])

        def rest_gate(r):
            return gate_t[:, TURNED:T] if r == 0 else gate_t[:, T + (r - 1) * REST : T + r * REST]

        turned = {}
        for h, (c0, c1) in enumerate(TURNED_PIECES):
            for r in range(TOP - 1):
                nc.scalar.activation(picked[c0, r][:], results(r + 1, c0 * P, c1 * P), ACT.Copy)
                for c in range(c0, c1):
                    turned[c, r] = bank[BLOCKS + 2 * h + r][:, (c - c0) * P : (c - c0 + 1) * P]
                    nc.tensor.transpose(turned[c, r], picked[c0, r][:, (c - c0) * P : (c - c0 + 1) * P], ident[:])
        rest_picked = [
            held.tile([P, c1 - c0], F32, name=f"rest_picked{c0}", tag=tag)
            for (c0, c1), tag in zip(REST_PIECES, ("rest_picked", "picked2_1"))
        ]

        def pick_rest(h):
            c0, c1 = REST_PIECES[h]
            nc.scalar.activation(rest_picked[h][:], results(TOP - 1, TURNED + c0, TURNED + c1), ACT.Copy)

        pick_rest(0)
        for c in range(BLOCKS):
            for r in range(TOP - 1):
                nc.scalar.activation(scaled[r][:, c, :], turned[c, r], ACT.Copy, scale=gate_cols[r][:, c : c + 1])
                nc.tensor.matmul(
                    bank[c][:, 0:P], scaled[r][:, c, :], ident[:], start=(r == 0), stop=(r == TOP - 2), is_transpose=True
                )
        pick_rest(1)

        for r in range(TOP - 1):
            nc.vector.tensor_tensor(rest_gated[r][:], results(r, TURNED, T), rest_gate(r), ALU.mult)
        nc.vector.tensor_tensor(fused[:], results(0, 0, TURNED), gate_t[:, 0:TURNED], ALU.mult)

        def add_pair(h):
            c0, c1 = REST_PIECES[h]
            nc.vector.tensor_tensor(rest_pair[:, c0:c1], rest_gated[0][:, c0:c1], rest_gated[1][:, c0:c1], ALU.add)

        third = [rest_gated[2][:, c0:c1] for c0, c1 in REST_PIECES]

        def product(h):
            c0, c1 = REST_PIECES[h]
            nc.vector.tensor_tensor(third[h], rest_picked[h][:], rest_gate(2)[:, c0:c1], ALU.mult)

        def store(t0, t1):
            nc.sync.dma_start(out=out[:, t0:t1], in_=out_t[:, t0:t1])

        def finish_rest(h):
            c0, c1 = REST_PIECES[h]
            nc.vector.tensor_tensor(out_t[:, TURNED + c0 : TURNED + c1], rest_pair[:, c0:c1], third[h], ALU.add)
            store(TURNED + c0, TURNED + c1)

        def finish_block(c):
            cols = slice(c * P, (c + 1) * P)
            nc.vector.tensor_tensor(out_t[:, cols], bank[c][:, 0:P], fused[:, cols], ALU.add)

        add_pair(0)
        product(0)
        add_pair(1)
        finish_rest(0)
        finish_block(0)
        product(1)
        finish_block(1)
        store(0, 2 * P)
        finish_rest(1)
        finish_block(2)
        store(2 * P, TURNED)
